import numpy as np
import ml_dtypes


def mxq(x, axis, fmt="e4m3"):
    dtype, down = {"e4m3": (ml_dtypes.float8_e4m3fn, 7), "e5m2": (ml_dtypes.float8_e5m2, 14)}[fmt]
    v = np.moveaxis(np.asarray(x, np.float32).astype(ml_dtypes.bfloat16).astype(np.float64), axis, -1)
    blocks = v.reshape(v.shape[:-1] + (-1, 32))
    amax = np.abs(blocks).max(-1, keepdims=True)
    byte = np.maximum(np.where(amax > 0, np.frexp(amax)[1] - 1 + 127, 0) - down, 1)
    scale = np.exp2(byte - 127.0)
    codes = (blocks / scale).astype(np.float32).astype(dtype).astype(np.float64)
    return np.moveaxis((codes * scale).reshape(v.shape), -1, axis)


WIDE = False


def mx_kscale(k):
    if not WIDE:
        return np.ones(k)
    levels = np.array([10, -10, 5, -5, 0])
    if k % 512:
        return np.exp2(np.random.permutation(np.resize(levels, k // 32))).repeat(32)
    a = np.empty((k // 512, 16))
    for p in range(k // 512):
        a[p, :8] = np.random.permutation(np.resize(levels, 8))
        for g in range(8):
            far = levels[np.abs(levels - a[p, g]) >= 10]
            a[p, g + 8] = far[np.random.randint(len(far))]
    return np.exp2(a.ravel()).repeat(32)


def f64(x):
    return np.asarray(x).astype(np.float64)


def striped(idx):
    return np.tile(idx.reshape(-1, 16).T, (8, 1)).astype(np.uint16)


def unstriped(offs):
    return offs[:16].T.reshape(-1).astype(np.int64)


E2M1 = np.array([0.0, 0.5, 1.0, 1.5, 2.0, 3.0, 4.0, 6.0, -0.0, -0.5, -1.0, -1.5, -2.0, -3.0, -4.0, -6.0])


def pack_weight(w, fmt):
    k, n = w.shape
    w = f64(np.asarray(w, np.float32).astype(ml_dtypes.bfloat16)).reshape(k // 32, 32, n)
    amax = np.abs(w).max(1)
    if fmt == "e4m3":
        byte = np.frexp(amax)[1] - 1 + 127 - 7
    else:
        mant, ex = np.frexp(amax / 6.0)
        byte = np.where(mant > 0.5, ex, ex - 1) + 127
    byte = np.clip(np.where(amax > 0, byte, 1), 1, 254)
    scaled = (w * np.exp2(127.0 - byte)[:, None, :]).reshape(k, n).astype(np.float32)
    by_word = np.ascontiguousarray(scaled.reshape(k // 512, 128, 4, n).transpose(0, 1, 3, 2))
    if fmt == "e4m3":
        words = by_word.astype(ml_dtypes.float8_e4m3fn).view(np.uint8)
    else:
        c = by_word.astype(ml_dtypes.float4_e2m1fn).view(np.uint8) & 0xF
        words = (c[..., 0::2] | (c[..., 1::2] << 4)).reshape(k // 512, 128, 2 * n)
    return np.ascontiguousarray(words), np.ascontiguousarray(byte.astype(np.uint8).reshape(k // 512, 16, n))


def unpack_weight(words, scales, fmt):
    g, _, n = scales.shape
    words = np.ascontiguousarray(words).reshape(g, 128, n, -1)
    if fmt == "e4m3":
        vals = words.view(ml_dtypes.float8_e4m3fn).astype(np.float64)
    else:
        nib = np.empty((g, 128, n, 4), np.uint8)
        nib[..., 0::2] = words & 0xF
        nib[..., 1::2] = words >> 4
        vals = E2M1[nib]
    vals = vals * np.repeat(np.exp2(scales.astype(np.float64) - 127.0), 8, axis=1)[..., None]
    return vals.transpose(0, 1, 3, 2).reshape(g * 512, n)


def planes(y):
    n, m = y.shape
    v = y.astype(np.float32).astype(ml_dtypes.bfloat16).astype(np.float64).reshape(n // 32, 32, m)
    top = np.abs(v).max(1)
    byte = np.clip(np.where(top > 0, np.frexp(top)[1] - 1 + 127 - 7, 1), 1, 254)
    codes = (v * np.exp2(127.0 - byte)[:, None, :]).reshape(n, m).astype(np.float32).astype(ml_dtypes.float8_e4m3fn).view(np.uint8)
    words = codes.reshape(n // 512, 128, 4, m).transpose(0, 1, 3, 2)
    return np.ascontiguousarray(words), np.ascontiguousarray(byte.astype(np.uint8).reshape(n // 512, 16, m))


def d_relu2(v):
    return 2.0 * np.maximum(v, 0.0)


K, T, E, C, H, N = 512, 640, 10, 128, 512, 1536


def by_expert(wq, xq):
    return np.concatenate([wq[e].T @ xq[:, e * C:(e + 1) * C] for e in range(E)], axis=1)


def setup_inputs():
    n = np.random.standard_normal
    v = mx_kscale(N)
    u = mx_kscale(H)
    first = np.random.permutation(np.repeat(np.arange(E), T // E))
    second = (first + 1 + np.random.permutation(np.repeat(np.arange(E - 1), -(-T // (E - 1)))[:T])) % E
    while np.bincount(second, minlength=E).max() != T // E:
        load = np.bincount(second, minlength=E); hi, lo = int(load.argmax()), int(load.argmin())
        t = np.flatnonzero((second == hi) & (first != lo))[0]; second[t] = lo
    slot_token = np.empty(E * C, np.int64); pos = np.empty((2, T), np.int64); fill = np.zeros(E, np.int64)
    place = np.stack([np.random.permutation(C) for _ in range(E)])
    for r, deal in enumerate((first, second)):
        for t in np.random.permutation(T):
            e = deal[t]; j = e * C + place[e, fill[e]]; fill[e] += 1; slot_token[j] = t; pos[r, t] = j
    g = np.random.uniform(0.2, 0.8, T)
    dy = pack_weight(n((N, T)) * v[:, None], "e4m3")
    return {
        "dy_words": dy[0],
        "dy_scales": dy[1],
        "w2t": (n((E, N, H)) / np.sqrt(N) / v[None, :, None] * u).astype(np.float32),
        "w1t": (n((H, K)) / np.sqrt(H) / u[:, None]).astype(np.float32),
        "a": (n((H, T))).astype(np.float32),
        "gate": np.stack([np.tile(g, (128, 1)), np.tile(1.0 - g, (128, 1))]).astype(np.float32),
        "offs": striped(slot_token),
        "pos1": striped(pos[0]),
        "pos2": striped(pos[1]),
    }


def reference(dy_words, dy_scales, w2t, w1t, a, gate, offs, pos1, pos2):
    w2tq = mxq(f64(w2t), 1, "e4m3")
    w1tq = mxq(f64(w1t), 0, "e4m3")
    idx = unstriped(offs)
    gq = unpack_weight(dy_words, dy_scales, "e4m3")[:, idx]
    y = by_expert(w2tq, gq)
    dh = sum(f64(gate[r, :1]) * y[:, unstriped(p)] for r, p in enumerate((pos1, pos2)))
    out_0 = w1tq.T @ mxq(dh * d_relu2(f64(a)), 0, "e4m3")
    return (out_0,) + planes(out_0)

@@ -1,0 +1,284 @@
+from contextlib import ExitStack
+
+import concourse.mybir as mybir
+from concourse.masks import make_identity
+
+K, T, E, C, H, N = 512, 640, 10, 128, 512, 1536
+FLOPS = 2 * E * C * N * H + 2 * T * H * K
+
+F32 = mybir.dt.float32
+BF16 = mybir.dt.bfloat16
+I32 = mybir.dt.int32
+U32 = mybir.dt.uint32
+U16 = mybir.dt.uint16
+U8 = mybir.dt.uint8
+FP8X4 = mybir.dt.float8_e4m3fn_x4
+MULT = mybir.AluOpType.mult
+RELU = mybir.ActivationFunctionType.Relu
+
+P = 128
+PACK = 4
+K_PASS = P * PACK
+PASSES = N // K_PASS
+PLANES = H // P
+SLOTS = E * C
+LIST_COL = 16
+GATHER = 2 * C
+CHUNKS = ((0, 2), (2, 2), (4, 1))
+
+
+def tile_moe_sub_relu2_kernel(
+    tc, dy_words, dy_scales, w2t, w1t, a, gate, offs, pos1, pos2, out_0, out_1, out_2
+):
+    nc = tc.nc
+    with ExitStack() as ctx:
+        keep = ctx.enter_context(tc.tile_pool(name="keep", bufs=1))
+        ring = ctx.enter_context(tc.tile_pool(name="ring", bufs=1))
+        psum = ctx.enter_context(tc.psum_pool(name="psum", bufs=1))
+
+        offs_sb = keep.tile([P, SLOTS // LIST_COL], U16, name="offs_sb")
+        pos_sb = [keep.tile([P, T // LIST_COL], U16, name="pos_sb%d" % r) for r in range(2)]
+        dy_word_sb = [keep.tile([P, T], I32, name="dy_word_sb%d" % s, align_bytes=64) for s in range(PASSES)]
+        dy_scale_sb = keep.tile([P, T], U8, name="dy_scale_sb", align_bytes=64)
+        gate_sb = [keep.tile([P, T], F32, name="gate_sb%d" % r) for r in range(2)]
+        ident = keep.tile([P, P], F32, name="ident")
+        y_sb = [keep.tile([P, SLOTS], F32, name="y_sb%d" % c, align_bytes=64) for c in range(PLANES)]
+        slope = [keep.tile([P, T // P, P], F32, name="slope%d" % c) for c in range(PLANES)]
+        da_rows = [keep.tile([P, nb, H], BF16, name="da_rows%d" % b0, align_bytes=64) for b0, nb in CHUNKS]
+        w1_grouped = keep.tile([P, PACK, P, PACK], BF16, name="w1_grouped", align_bytes=64)
+        w1_codes = keep.tile([P, K], U32, name="w1_codes", align_bytes=64)
+        w1_scales = keep.tile([P, K], U8, name="w1_scales", align_bytes=64)
+        out_codes = keep.tile([P, T], I32, name="out_codes", align_bytes=64)
+        out_scales = keep.tile([P, T], U8, name="out_scales", align_bytes=64)
+
+        def raw_tile(shape):
+            return ring.tile(shape, F32, name="raw", bufs=8, align_bytes=64)
+
+        def load_w2(raw, e, s, c0, planes):
+            rows = w2t[e, s * K_PASS : (s + 1) * K_PASS, :].rearrange("(p j) h -> p j h", j=PACK)
+            nc.sync.dma_start(out=raw, in_=rows[:, :, c0 * P : (c0 + planes) * P])
+
+        def mx_tiles(words, lodging):
+            if lodging is None:
+                grouped = ring.tile([P, words * PACK], BF16, name="grouped", bufs=6, align_bytes=64)
+            else:
+                grouped = keep.tile([P, words * PACK], BF16, name="early", tag=lodging, align_bytes=64)
+            codes = ring.tile([P, words], U32, name="codes", bufs=12, align_bytes=64)
+            scales = ring.tile([P, words], U8, name="scales", bufs=12, align_bytes=64)
+            return grouped, codes, scales
+
+        def round_and_quantize(raw, grouped, codes, scales, on_vector):
+            passes = raw.shape[1]
+            dst = grouped.rearrange("p (s c i j) -> p s c j i", s=passes, i=4, j=PACK)
+            src = raw.rearrange("p s j (c i) -> p s c j i", i=4)
+            if on_vector:
+                nc.vector.tensor_copy(out=dst, in_=src)
+            else:
+                nc.scalar.copy(out=dst, in_=src)
+            nc.vector.quantize_mx(out=codes.bitcast(FP8X4), scales=scales, in_=grouped)
+
+        def load_piece(e, c):
+            raw = raw_tile([P, PASSES, PACK, P])
+            for s in range(PASSES):
+                load_w2(raw[:, s], e, s, c, 1)
+            return raw
+
+        def plane_piece(raw, steps, lodging):
+            grouped, codes, scales = mx_tiles(PASSES * P, lodging)
+            for s0, s1, on_vector in steps:
+                round_and_quantize(
+                    raw[:, s0:s1],
+                    grouped[:, s0 * K_PASS : s1 * K_PASS],
+                    codes[:, s0 * P : s1 * P],
+                    scales[:, s0 * P : s1 * P],
+                    on_vector,
+                )
+            return [(codes[:, s * P : (s + 1) * P], scales[:, s * P : (s + 1) * P]) for s in range(PASSES)]
+
+        gathered = {}
+
+        def gather_dy(g):
+            offsets = offs_sb[:, g * GATHER // LIST_COL : (g + 1) * GATHER // LIST_COL]
+            words = keep.tile([P, PASSES, GATHER], U32, name="slot_words", tag="slots%d" % g, align_bytes=64)
+            for s in range(PASSES):
+                nc.vector.tensor_copy(out=words[:, s, :], in_=dy_word_sb[s][:].bitcast(U32).indirect(offsets))
+            z = keep.tile([P, GATHER], U8, name="slot_scales%d" % g, align_bytes=64)
+            nc.vector.tensor_copy(out=z[:], in_=dy_scale_sb[:].indirect(offsets))
+            gathered[g] = (words, z)
+
+        def multiply(e, acc, quantized):
+            words, z = gathered[e * C // GATHER]
+            cols = slice(e * C % GATHER, e * C % GATHER + C)
+            for s in range(PASSES):
+                codes, scales = quantized[s]
+                nc.tensor.matmul_mx(
+                    out=acc,
+                    lhsT=codes.bitcast(FP8X4),
+                    lhsT_scale=scales,
+                    rhs=words[:, s, cols].bitcast(FP8X4),
+                    rhs_scale=z[4 * s : P, cols],
+                    start=(s == 0),
+                    stop=(s == PASSES - 1),
+                )
+
+        def make_slope(c):
+            a_sb = raw_tile([P, T])
+            nc.sync.dma_start(out=a_sb[:], in_=a[c * P : (c + 1) * P, :])
+            for b0, nb in CHUNKS:
+                turned = psum.tile([P, PLANES, P], F32, name="turned", bufs=3)
+                for b in range(nb):
+                    nc.tensor.transpose(turned[:, b, :], a_sb[:, (b0 + b) * P : (b0 + b + 1) * P], ident[:])
+                nc.scalar.activation(out=slope[c][:, b0 : b0 + nb, :], in_=turned[:, 0:nb, :], func=RELU, scale=2.0)
+
+        def fetch(c, b0, nb):
+            parts = []
+            for r in range(2):
+                part = ring.tile([P, nb * P], F32, name="part", bufs=4)
+                offsets = pos_sb[r][:, b0 * P // LIST_COL : (b0 + nb) * P // LIST_COL]
+                nc.vector.tensor_tensor(
+                    out=part[:], in0=y_sb[c][:].indirect(offsets), in1=gate_sb[r][:, b0 * P : (b0 + nb) * P], op=MULT
+                )
+                parts.append(part)
+            return parts
+
+        def combine(c, k, parts, first):
+            b0, nb = CHUNKS[k]
+            turned = psum.tile([P, PLANES, P], F32, name="turned", bufs=3)
+            for b in range(nb):
+                for r in range(2):
+                    nc.tensor.matmul(
+                        turned[:, b, :],
+                        lhsT=parts[r][:, (b0 - first + b) * P : (b0 - first + b + 1) * P],
+                        rhs=ident[:],
+                        start=(r == 0),
+                        stop=(r == 1),
+                        is_transpose=True,
+                    )
+            nc.vector.tensor_tensor(
+                out=da_rows[k][:, :, c * P : (c + 1) * P],
+                in0=turned[:, 0:nb, :],
+                in1=slope[c][:, b0 : b0 + nb, :],
+                op=MULT,
+            )
+
+        def quantize_w1():
+            for q in range(PACK):
+                raw = raw_tile([P, PACK, P])
+                rows = w1t.rearrange("(p j) k -> p j k", j=PACK)
+                nc.sync.dma_start(out=raw[:], in_=rows[:, :, q * P : (q + 1) * P])
+                nc.scalar.copy(
+                    out=w1_grouped[:, :, q * 32 : (q + 1) * 32, :].rearrange("p t m j -> p m j t"),
+                    in_=raw[:].rearrange("p j (m t) -> p m j t", t=PACK),
+                )
+            nc.vector.quantize_mx(
+                out=w1_codes[:].bitcast(FP8X4),
+                scales=w1_scales[:],
+                in_=w1_grouped[:].rearrange("p t m j -> p (t m j)"),
+            )
+
+        def finish(k):
+            b0, nb = CHUNKS[k]
+            width = nb * P
+            cols = slice(b0 * P, b0 * P + width)
+            back = psum.tile([P, 2, 2, P], F32, name="turned", bufs=3)
+            words = da_rows[k][:].bitcast(F32)
+            for b in range(nb):
+                for u in range(2):
+                    nc.tensor.transpose(back[:, b, u, :], words[:, b, u : H // 2 : 2], ident[:])
+            da_grouped = ring.tile([P, width * PACK], BF16, name="da_grouped", bufs=3, align_bytes=64)
+            nc.scalar.copy(
+                out=da_grouped[:].bitcast(F32).rearrange("p (b n u) -> p b n u", b=nb, u=2),
+                in_=back[:, 0:nb, :, :].rearrange("p b u n -> p b n u"),
+            )
+            da_codes = ring.tile([P, width], U32, name="da_codes", bufs=3, align_bytes=64)
+            da_scales = ring.tile([P, width], U8, name="da_scales", bufs=3, align_bytes=64)
+            nc.vector.quantize_mx(out=da_codes[:].bitcast(FP8X4), scales=da_scales[:], in_=da_grouped[:])
+            result = ring.tile([P, PACK, width], F32, name="result", bufs=3, align_bytes=64)
+            rounded = ring.tile([P, width, PACK], BF16, name="rounded", bufs=3, align_bytes=64)
+            for b in range(nb):
+                bank = psum.tile([P, PACK, P], F32, name="bank", bufs=3)
+                for t in range(PACK):
+                    nc.tensor.matmul_mx(
+                        out=bank[:, t, :],
+                        lhsT=w1_codes[:, t * P : (t + 1) * P].bitcast(FP8X4),
+                        lhsT_scale=w1_scales[:, t * P : (t + 1) * P],
+                        rhs=da_codes[:, b * P : (b + 1) * P].bitcast(FP8X4),
+                        rhs_scale=da_scales[:, b * P : (b + 1) * P],
+                        start=True,
+                        stop=True,
+                    )
+                if k == len(CHUNKS) - 1:
+                    nc.vector.tensor_copy(
+                        out=rounded[:, b * P : (b + 1) * P, :], in_=bank[:].rearrange("p t n -> p n t")
+                    )
+                nc.scalar.copy(out=result[:, :, b * P : (b + 1) * P], in_=bank[:])
+            if k < len(CHUNKS) - 1:
+                nc.vector.tensor_copy(
+                    out=rounded[:].rearrange("p (c i) t -> p c t i", i=4),
+                    in_=result[:].rearrange("p t (c i) -> p c t i", i=4),
+                )
+            nc.vector.quantize_mx(
+                out=out_codes[:, cols].bitcast(FP8X4),
+                scales=out_scales[:, cols],
+                in_=rounded[:].rearrange("p n t -> p (n t)"),
+            )
+            nc.sync.dma_start(out=out_0.rearrange("(p t) n -> p t n", t=PACK)[:, :, cols], in_=result[:])
+            nc.sync.dma_start(
+                out=out_1[0].rearrange("p n d -> p (n d)").bitcast(I32)[:, cols], in_=out_codes[:, cols]
+            )
+
+        nc.sync.dma_start(offs_sb[:], offs)
+        first_raw = load_piece(0, 0)
+        for s in range(PASSES):
+            nc.sync.dma_start(out=dy_word_sb[s][:], in_=dy_words[s].rearrange("p n d -> p (n d)").bitcast(I32))
+        nc.gpsimd.memset(dy_scale_sb[:].bitcast(I32), 0)
+        for q in range(4):
+            nc.sync.dma_start(
+                out=dy_scale_sb[32 * q : 32 * q + 4 * PASSES, :].bitcast(I32),
+                in_=dy_scales[:, 4 * q : 4 * q + 4, :].bitcast(I32),
+            )
+        make_identity(nc, ident[:])
+
+        for c in range(PLANES):
+            groups = ((0, 4), (4, 8), (8, 10)) if c < PLANES - 1 else ((0, 4), (4, 8), (8, 9), (9, 10))
+            for e0, e1 in groups:
+                acc = psum.tile([P, 4 * C], F32, name="acc", bufs=2)
+                for e in range(e0, e1):
+                    raw = first_raw if (c, e) == (0, 0) else load_piece(e, c)
+                    if (c, e) == (PLANES - 1, E - 1):
+                        steps = ((0, 1, False), (1, 2, False), (2, 3, True))
+                    elif c == 0 or e < 4:
+                        steps = ((0, 2, False), (2, 3, False))
+                    else:
+                        steps = ((0, 1, False), (1, 3, True))
+                    lodging = "slots%d" % (e // 2 + 1) if c == 0 and e % 2 == 1 and e < E - 1 else None
+                    quantized = plane_piece(raw, steps, lodging)
+                    if c == 0 and e * C % GATHER == 0:
+                        gather_dy(e * C // GATHER)
+                    multiply(e, acc[:, (e - e0) * C : (e - e0 + 1) * C], quantized)
+                    if e == E // 2 and c < PLANES - 1:
+                        make_slope(c)
+                    if (c, e) == (0, E // 2):
+                        nc.sync.dma_start(pos_sb[0][:], pos1)
+                        nc.sync.dma_start(pos_sb[1][:], pos2)
+                        for r in range(2):
+                            nc.sync.dma_start(out=gate_sb[r][:], in_=gate[r])
+                nc.scalar.copy(out=y_sb[c][:, e0 * C : e1 * C], in_=acc[:, 0 : (e1 - e0) * C])
+            if c < PLANES - 1:
+                parts = fetch(c, 0, T // P)
+                for k in range(len(CHUNKS)):
+                    combine(c, k, parts, 0)
+
+        make_slope(PLANES - 1)
+        quantize_w1()
+        c0, planes = PLANES - 1, 1
+        for k in range(len(CHUNKS)):
+            b0, nb = CHUNKS[k]
+            for c in range(c0, c0 + planes):
+                combine(c, k, fetch(c, b0, nb), b0)
+            finish(k)
+        for q in range(4):
+            queue = nc.sync if q % 2 == 0 else nc.scalar
+            queue.dma_start(
+                out=out_2[0, 4 * q : 4 * q + 4, :].bitcast(I32), in_=out_scales[32 * q : 32 * q + 4, :].bitcast(I32)
+            )

@@ -25,6 +25,8 @@ SLOTS = E * C
 LIST_COL = 16
 GATHER = 2 * C
 CHUNKS = ((0, 2), (2, 2), (4, 1))
+LATE = 0
+BANK = 512
 
 
 def tile_moe_sub_relu2_kernel(
@@ -40,12 +42,10 @@ def tile_moe_sub_relu2_kernel(
         pos_sb = [keep.tile([P, T // LIST_COL], U16, name="pos_sb%d" % r) for r in range(2)]
         dy_word_sb = [keep.tile([P, T], I32, name="dy_word_sb%d" % s, align_bytes=64) for s in range(PASSES)]
         dy_scale_sb = keep.tile([P, T], U8, name="dy_scale_sb", align_bytes=64)
-        gate_sb = [keep.tile([P, T], F32, name="gate_sb%d" % r) for r in range(2)]
         ident = keep.tile([P, P], F32, name="ident")
         y_sb = [keep.tile([P, SLOTS], F32, name="y_sb%d" % c, align_bytes=64) for c in range(PLANES)]
-        slope = [keep.tile([P, T // P, P], F32, name="slope%d" % c) for c in range(PLANES)]
+        slope = [keep.tile([P, H], F32, name="slope%d" % b) for b in range(T // P)]
         da_rows = [keep.tile([P, nb, H], BF16, name="da_rows%d" % b0, align_bytes=64) for b0, nb in CHUNKS]
-        w1_grouped = keep.tile([P, PACK, P, PACK], BF16, name="w1_grouped", align_bytes=64)
         w1_codes = keep.tile([P, K], U32, name="w1_codes", align_bytes=64)
         w1_scales = keep.tile([P, K], U8, name="w1_scales", align_bytes=64)
         out_codes = keep.tile([P, T], I32, name="out_codes", align_bytes=64)
@@ -60,40 +60,21 @@ def tile_moe_sub_relu2_kernel(
 
         def mx_tiles(words, lodging):
             if lodging is None:
-                grouped = ring.tile([P, words * PACK], BF16, name="grouped", bufs=6, align_bytes=64)
+                grouped = ring.tile([P, words * PACK], BF16, name="grouped", bufs=5, align_bytes=64)
             else:
                 grouped = keep.tile([P, words * PACK], BF16, name="early", tag=lodging, align_bytes=64)
-            codes = ring.tile([P, words], U32, name="codes", bufs=12, align_bytes=64)
-            scales = ring.tile([P, words], U8, name="scales", bufs=12, align_bytes=64)
+            codes = ring.tile([P, words], U32, name="codes", bufs=9, align_bytes=64)
+            scales = ring.tile([P, words], U8, name="scales", bufs=9, align_bytes=64)
             return grouped, codes, scales
 
         def round_and_quantize(raw, grouped, codes, scales, on_vector):
-            passes = raw.shape[1]
-            dst = grouped.rearrange("p (s c i j) -> p s c j i", s=passes, i=4, j=PACK)
-            src = raw.rearrange("p s j (c i) -> p s c j i", i=4)
+            dst = grouped.rearrange("p (c i j) -> p c j i", i=4, j=PACK)
+            src = raw.rearrange("p j (c i) -> p c j i", i=4)
             if on_vector:
                 nc.vector.tensor_copy(out=dst, in_=src)
             else:
                 nc.scalar.copy(out=dst, in_=src)
             nc.vector.quantize_mx(out=codes.bitcast(FP8X4), scales=scales, in_=grouped)
-
-        def load_piece(e, c):
-            raw = raw_tile([P, PASSES, PACK, P])
-            for s in range(PASSES):
-                load_w2(raw[:, s], e, s, c, 1)
-            return raw
-
-        def plane_piece(raw, steps, lodging):
-            grouped, codes, scales = mx_tiles(PASSES * P, lodging)
-            for s0, s1, on_vector in steps:
-                round_and_quantize(
-                    raw[:, s0:s1],
-                    grouped[:, s0 * K_PASS : s1 * K_PASS],
-                    codes[:, s0 * P : s1 * P],
-                    scales[:, s0 * P : s1 * P],
-                    on_vector,
-                )
-            return [(codes[:, s * P : (s + 1) * P], scales[:, s * P : (s + 1) * P]) for s in range(PASSES)]
 
         gathered = {}
 
@@ -106,34 +87,82 @@ def tile_moe_sub_relu2_kernel(
             nc.vector.tensor_copy(out=z[:], in_=dy_scale_sb[:].indirect(offsets))
             gathered[g] = (words, z)
 
-        def multiply(e, acc, quantized):
+        def multiply(e, s, acc, codes, scales):
             words, z = gathered[e * C // GATHER]
             cols = slice(e * C % GATHER, e * C % GATHER + C)
-            for s in range(PASSES):
-                codes, scales = quantized[s]
-                nc.tensor.matmul_mx(
-                    out=acc,
-                    lhsT=codes.bitcast(FP8X4),
-                    lhsT_scale=scales,
-                    rhs=words[:, s, cols].bitcast(FP8X4),
-                    rhs_scale=z[4 * s : P, cols],
-                    start=(s == 0),
-                    stop=(s == PASSES - 1),
-                )
+            nc.tensor.matmul_mx(
+                out=acc,
+                lhsT=codes.bitcast(FP8X4),
+                lhsT_scale=scales,
+                rhs=words[:, s, cols].bitcast(FP8X4),
+                rhs_scale=z[4 * s : P, cols],
+                start=(s == 0),
+                stop=(s == PASSES - 1),
+            )
 
-        def make_slope(c):
-            a_sb = raw_tile([P, T])
-            nc.sync.dma_start(out=a_sb[:], in_=a[c * P : (c + 1) * P, :])
-            for b0, nb in CHUNKS:
-                turned = psum.tile([P, PLANES, P], F32, name="turned", bufs=3)
-                for b in range(nb):
-                    nc.tensor.transpose(turned[:, b, :], a_sb[:, (b0 + b) * P : (b0 + b + 1) * P], ident[:])
-                nc.scalar.activation(out=slope[c][:, b0 : b0 + nb, :], in_=turned[:, 0:nb, :], func=RELU, scale=2.0)
+        def expert_group(e0, e1, c0, planes, preloaded):
+            width = planes * P
+            accs = [psum.tile([P, BANK], F32, name="acc", bufs=4) for c in range(planes)]
+            for e in range(e0, e1):
+                slots = slice((e - e0) * C, (e - e0 + 1) * C)
+                for s in range(PASSES):
+                    if (e, s) in preloaded:
+                        raw = preloaded[e, s]
+                    else:
+                        raw = raw_tile([P, PACK, width])
+                        load_w2(raw[:], e, s, c0, planes)
+                    g = e * C // GATHER
+                    lodging = "slots%d" % (g + 1) if c0 == 0 and e % 2 == 1 and s == 0 and e < E - 1 else None
+                    grouped, codes, scales = mx_tiles(width, lodging)
+                    if (e, s, c0 + planes) == (E - 1, PASSES - 1, PLANES):
+                        for c in range(planes):
+                            cols = slice(c * P, (c + 1) * P)
+                            round_and_quantize(
+                                raw[:, :, cols],
+                                grouped[:, c * K_PASS : (c + 1) * K_PASS],
+                                codes[:, cols],
+                                scales[:, cols],
+                                c == 0,
+                            )
+                            multiply(e, s, accs[c][:, slots], codes[:, cols], scales[:, cols])
+                            copy = nc.vector.tensor_copy if c == 0 else nc.scalar.copy
+                            copy(out=y_sb[c0 + c][:, e0 * C : e1 * C], in_=accs[c][:, 0 : (e1 - e0) * C])
+                        return
+                    round_and_quantize(raw[:], grouped[:], codes[:], scales[:], s == PASSES - 1 or (s == 1 and e >= E - 2 and not LATE))
+                    if g not in gathered:
+                        gather_dy(g)
+                    for c in range(planes):
+                        cols = slice(c * P, (c + 1) * P)
+                        multiply(e, s, accs[c][:, slots], codes[:, cols], scales[:, cols])
+            for c in range(planes):
+                nc.scalar.copy(out=y_sb[c0 + c][:, e0 * C : e1 * C], in_=accs[c][:, 0 : (e1 - e0) * C])
+
+        gate_sb = []
+
+        def load_gates():
+            for r in range(2):
+                tile = raw_tile([P, T])
+                nc.sync.dma_start(out=tile[:], in_=gate[r])
+                gate_sb.append(tile)
+
+        def make_slopes(c0, planes):
+            a_sb = []
+            for c in range(c0, c0 + planes):
+                tile = raw_tile([P, T])
+                nc.sync.dma_start(out=tile[:], in_=a[c * P : (c + 1) * P, :])
+                a_sb.append(tile)
+            for b in range(T // P):
+                turned = psum.tile([P, BANK], F32, name="acc", bufs=4)
+                for c in range(planes):
+                    nc.tensor.transpose(turned[:, c * P : (c + 1) * P], a_sb[c][:, b * P : (b + 1) * P], ident[:])
+                nc.scalar.activation(
+                    out=slope[b][:, c0 * P : (c0 + planes) * P], in_=turned[:, 0 : planes * P], func=RELU, scale=2.0
+                )
 
         def fetch(c, b0, nb):
             parts = []
             for r in range(2):
-                part = ring.tile([P, nb * P], F32, name="part", bufs=4)
+                part = ring.tile([P, nb * P], F32, name="part", bufs=6)
                 offsets = pos_sb[r][:, b0 * P // LIST_COL : (b0 + nb) * P // LIST_COL]
                 nc.vector.tensor_tensor(
                     out=part[:], in0=y_sb[c][:].indirect(offsets), in1=gate_sb[r][:, b0 * P : (b0 + nb) * P], op=MULT
@@ -141,46 +170,42 @@ def tile_moe_sub_relu2_kernel(
                 parts.append(part)
             return parts
 
-        def combine(c, k, parts, first):
+        def combine(k, c0, planes):
             b0, nb = CHUNKS[k]
-            turned = psum.tile([P, PLANES, P], F32, name="turned", bufs=3)
+            turned = [psum.tile([P, BANK], F32, name="turned", bufs=2) for b in range(nb)]
+            for c in range(planes):
+                parts = fetch(c0 + c, b0, nb)
+                for b in range(nb):
+                    for r in range(2):
+                        nc.tensor.matmul(
+                            turned[b][:, c * P : (c + 1) * P],
+                            lhsT=parts[r][:, b * P : (b + 1) * P],
+                            rhs=ident[:],
+                            start=(r == 0),
+                            stop=(r == 1),
+                            is_transpose=True,
+                        )
             for b in range(nb):
-                for r in range(2):
-                    nc.tensor.matmul(
-                        turned[:, b, :],
-                        lhsT=parts[r][:, (b0 - first + b) * P : (b0 - first + b + 1) * P],
-                        rhs=ident[:],
-                        start=(r == 0),
-                        stop=(r == 1),
-                        is_transpose=True,
-                    )
-            nc.vector.tensor_tensor(
-                out=da_rows[k][:, :, c * P : (c + 1) * P],
-                in0=turned[:, 0:nb, :],
-                in1=slope[c][:, b0 : b0 + nb, :],
-                op=MULT,
-            )
+                cols = slice(c0 * P, (c0 + planes) * P)
+                nc.vector.tensor_tensor(
+                    out=da_rows[k][:, b, cols], in0=turned[b][:, 0 : planes * P], in1=slope[b0 + b][:, cols], op=MULT
+                )
 
         def quantize_w1():
-            for q in range(PACK):
-                raw = raw_tile([P, PACK, P])
-                rows = w1t.rearrange("(p j) k -> p j k", j=PACK)
-                nc.sync.dma_start(out=raw[:], in_=rows[:, :, q * P : (q + 1) * P])
-                nc.scalar.copy(
-                    out=w1_grouped[:, :, q * 32 : (q + 1) * 32, :].rearrange("p t m j -> p m j t"),
-                    in_=raw[:].rearrange("p j (m t) -> p m j t", t=PACK),
-                )
-            nc.vector.quantize_mx(
-                out=w1_codes[:].bitcast(FP8X4),
-                scales=w1_scales[:],
-                in_=w1_grouped[:].rearrange("p t m j -> p (t m j)"),
+            raw = raw_tile([P, PACK, K])
+            nc.sync.dma_start(out=raw[:], in_=w1t.rearrange("(p j) k -> p j k", j=PACK))
+            grouped = ring.tile([P, K * PACK], BF16, name="grouped", bufs=5, align_bytes=64)
+            nc.scalar.copy(
+                out=grouped[:].rearrange("p (t m j) -> p m j t", t=PACK, j=PACK),
+                in_=raw[:].rearrange("p j (m t) -> p m j t", t=PACK),
             )
+            nc.vector.quantize_mx(out=w1_codes[:].bitcast(FP8X4), scales=w1_scales[:], in_=grouped[:])
 
         def finish(k):
             b0, nb = CHUNKS[k]
             width = nb * P
             cols = slice(b0 * P, b0 * P + width)
-            back = psum.tile([P, 2, 2, P], F32, name="turned", bufs=3)
+            back = psum.tile([P, 2, 2, P], F32, name="back", bufs=2)
             words = da_rows[k][:].bitcast(F32)
             for b in range(nb):
                 for u in range(2):
@@ -196,7 +221,7 @@ def tile_moe_sub_relu2_kernel(
             result = ring.tile([P, PACK, width], F32, name="result", bufs=3, align_bytes=64)
             rounded = ring.tile([P, width, PACK], BF16, name="rounded", bufs=3, align_bytes=64)
             for b in range(nb):
-                bank = psum.tile([P, PACK, P], F32, name="bank", bufs=3)
+                bank = psum.tile([P, PACK, P], F32, name="acc", bufs=4)
                 for t in range(PACK):
                     nc.tensor.matmul_mx(
                         out=bank[:, t, :],
@@ -207,16 +232,9 @@ def tile_moe_sub_relu2_kernel(
                         start=True,
                         stop=True,
                     )
-                if k == len(CHUNKS) - 1:
-                    nc.vector.tensor_copy(
-                        out=rounded[:, b * P : (b + 1) * P, :], in_=bank[:].rearrange("p t n -> p n t")
-                    )
+                copy = nc.vector.tensor_copy if k == len(CHUNKS) - 1 else nc.scalar.copy
+                copy(out=rounded[:, b * P : (b + 1) * P, :], in_=bank[:].rearrange("p t n -> p n t"))
                 nc.scalar.copy(out=result[:, :, b * P : (b + 1) * P], in_=bank[:])
-            if k < len(CHUNKS) - 1:
-                nc.vector.tensor_copy(
-                    out=rounded[:].rearrange("p (c i) t -> p c t i", i=4),
-                    in_=result[:].rearrange("p t (c i) -> p c t i", i=4),
-                )
             nc.vector.quantize_mx(
                 out=out_codes[:, cols].bitcast(FP8X4),
                 scales=out_scales[:, cols],
@@ -228,7 +246,11 @@ def tile_moe_sub_relu2_kernel(
             )
 
         nc.sync.dma_start(offs_sb[:], offs)
-        first_raw = load_piece(0, 0)
+        first = {}
+        for s in range(PASSES):
+            first[0, s] = raw_tile([P, PACK, H])
+            if s < 2:
+                load_w2(first[0, s][:], 0, s, 0, PLANES)
         for s in range(PASSES):
             nc.sync.dma_start(out=dy_word_sb[s][:], in_=dy_words[s].rearrange("p n d -> p (n d)").bitcast(I32))
         nc.gpsimd.memset(dy_scale_sb[:].bitcast(I32), 0)
@@ -237,45 +259,29 @@ def tile_moe_sub_relu2_kernel(
                 out=dy_scale_sb[32 * q : 32 * q + 4 * PASSES, :].bitcast(I32),
                 in_=dy_scales[:, 4 * q : 4 * q + 4, :].bitcast(I32),
             )
+        load_w2(first[0, 2][:], 0, 2, 0, PLANES)
         make_identity(nc, ident[:])
 
-        for c in range(PLANES):
-            groups = ((0, 4), (4, 8), (8, 10)) if c < PLANES - 1 else ((0, 4), (4, 8), (8, 9), (9, 10))
-            for e0, e1 in groups:
-                acc = psum.tile([P, 4 * C], F32, name="acc", bufs=2)
-                for e in range(e0, e1):
-                    raw = first_raw if (c, e) == (0, 0) else load_piece(e, c)
-                    if (c, e) == (PLANES - 1, E - 1):
-                        steps = ((0, 1, False), (1, 2, False), (2, 3, True))
-                    elif c == 0 or e < 4:
-                        steps = ((0, 2, False), (2, 3, False))
-                    else:
-                        steps = ((0, 1, False), (1, 3, True))
-                    lodging = "slots%d" % (e // 2 + 1) if c == 0 and e % 2 == 1 and e < E - 1 else None
-                    quantized = plane_piece(raw, steps, lodging)
-                    if c == 0 and e * C % GATHER == 0:
-                        gather_dy(e * C // GATHER)
-                    multiply(e, acc[:, (e - e0) * C : (e - e0 + 1) * C], quantized)
-                    if e == E // 2 and c < PLANES - 1:
-                        make_slope(c)
-                    if (c, e) == (0, E // 2):
-                        nc.sync.dma_start(pos_sb[0][:], pos1)
-                        nc.sync.dma_start(pos_sb[1][:], pos2)
-                        for r in range(2):
-                            nc.sync.dma_start(out=gate_sb[r][:], in_=gate[r])
-                nc.scalar.copy(out=y_sb[c][:, e0 * C : e1 * C], in_=acc[:, 0 : (e1 - e0) * C])
-            if c < PLANES - 1:
-                parts = fetch(c, 0, T // P)
-                for k in range(len(CHUNKS)):
-                    combine(c, k, parts, 0)
-
-        make_slope(PLANES - 1)
+        expert_group(0, 4, 0, PLANES, first)
+        nc.sync.dma_start(pos_sb[0][:], pos1)
+        nc.sync.dma_start(pos_sb[1][:], pos2)
+        expert_group(4, 8, 0, PLANES, {})
+        c0 = 0
+        if LATE:
+            load_gates()
+            make_slopes(0, 2)
+            expert_group(8, 10, 0, 2, {})
+            for k in range(len(CHUNKS)):
+                combine(k, 0, 2)
+            c0 = 2
+        expert_group(8, 9, c0, PLANES - c0, {})
+        expert_group(9, 10, c0, PLANES - c0, {})
+        if not LATE:
+            load_gates()
+        make_slopes(c0, PLANES - c0)
         quantize_w1()
-        c0, planes = PLANES - 1, 1
         for k in range(len(CHUNKS)):
-            b0, nb = CHUNKS[k]
-            for c in range(c0, c0 + planes):
-                combine(c, k, fetch(c, b0, nb), b0)
+            combine(k, c0, PLANES - c0)
             finish(k)
         for q in range(4):
             queue = nc.sync if q % 2 == 0 else nc.scalar

@@ -25,7 +25,9 @@ SLOTS = E * C
 LIST_COL = 16
 GATHER = 2 * C
 CHUNKS = ((0, 2), (2, 2), (4, 1))
-LATE = 0
+BLOCKS = T // P
+HALF = PLANES // 2
+WHOLE_EXPERTS = 8
 BANK = 512
 
 
@@ -44,6 +46,8 @@ def tile_moe_sub_relu2_kernel(
         dy_scale_sb = keep.tile([P, T], U8, name="dy_scale_sb", align_bytes=64)
         ident = keep.tile([P, P], F32, name="ident")
         y_sb = [keep.tile([P, SLOTS], F32, name="y_sb%d" % c, align_bytes=64) for c in range(PLANES)]
+        gate_cols = keep.tile([P, 2 * BLOCKS], F32, name="gate_cols")
+        gate_sb = [keep.tile([P, T], F32, name="gate_sb%d" % r) for r in range(2)]
         slope = [keep.tile([P, H], F32, name="slope%d" % b) for b in range(T // P)]
         da_rows = [keep.tile([P, nb, H], BF16, name="da_rows%d" % b0, align_bytes=64) for b0, nb in CHUNKS]
         w1_codes = keep.tile([P, K], U32, name="w1_codes", align_bytes=64)
@@ -55,16 +59,22 @@ def tile_moe_sub_relu2_kernel(
             return ring.tile(shape, F32, name="raw", bufs=8, align_bytes=64)
 
         def load_w2(raw, e, s, c0, planes):
-            rows = w2t[e, s * K_PASS : (s + 1) * K_PASS, :].rearrange("(p j) h -> p j h", j=PACK)
-            nc.sync.dma_start(out=raw, in_=rows[:, :, c0 * P : (c0 + planes) * P])
+            rows = w2t[e, s * K_PASS : (s + 1) * K_PASS, :]
+            if planes == PLANES:
+                nc.sync.dma_start(
+                    out=raw.rearrange("p j h -> p (j h)"), in_=rows.rearrange("(p j) h -> p (j h)", j=PACK)
+                )
+            else:
+                rows = rows.rearrange("(p j) h -> p j h", j=PACK)
+                nc.sync.dma_start(out=raw, in_=rows[:, :, c0 * P : (c0 + planes) * P])
 
         def mx_tiles(words, lodging):
             if lodging is None:
-                grouped = ring.tile([P, words * PACK], BF16, name="grouped", bufs=5, align_bytes=64)
+                grouped = ring.tile([P, words * PACK], BF16, name="grouped", bufs=6, align_bytes=64)
             else:
                 grouped = keep.tile([P, words * PACK], BF16, name="early", tag=lodging, align_bytes=64)
-            codes = ring.tile([P, words], U32, name="codes", bufs=9, align_bytes=64)
-            scales = ring.tile([P, words], U8, name="scales", bufs=9, align_bytes=64)
+            codes = ring.tile([P, words], U32, name="codes", bufs=7, align_bytes=64)
+            scales = ring.tile([P, words], U8, name="scales", bufs=7, align_bytes=64)
             return grouped, codes, scales
 
         def round_and_quantize(raw, grouped, codes, scales, on_vector):
@@ -114,7 +124,7 @@ def tile_moe_sub_relu2_kernel(
                     g = e * C // GATHER
                     lodging = "slots%d" % (g + 1) if c0 == 0 and e % 2 == 1 and s == 0 and e < E - 1 else None
                     grouped, codes, scales = mx_tiles(width, lodging)
-                    if (e, s, c0 + planes) == (E - 1, PASSES - 1, PLANES):
+                    if (e, s) == (E - 1, PASSES - 1):
                         for c in range(planes):
                             cols = slice(c * P, (c + 1) * P)
                             round_and_quantize(
@@ -128,7 +138,7 @@ def tile_moe_sub_relu2_kernel(
                             copy = nc.vector.tensor_copy if c == 0 else nc.scalar.copy
                             copy(out=y_sb[c0 + c][:, e0 * C : e1 * C], in_=accs[c][:, 0 : (e1 - e0) * C])
                         return
-                    round_and_quantize(raw[:], grouped[:], codes[:], scales[:], s == PASSES - 1 or (s == 1 and e >= E - 2 and not LATE))
+                    round_and_quantize(raw[:], grouped[:], codes[:], scales[:], c0 == 0 and (PASSES * e + s) % 2 == 0)
                     if g not in gathered:
                         gather_dy(g)
                     for c in range(planes):
@@ -137,64 +147,75 @@ def tile_moe_sub_relu2_kernel(
             for c in range(planes):
                 nc.scalar.copy(out=y_sb[c0 + c][:, e0 * C : e1 * C], in_=accs[c][:, 0 : (e1 - e0) * C])
 
-        gate_sb = []
+        def aux_bank(shape):
+            return psum.tile(shape, F32, name="aux", bufs=4)
 
-        def load_gates():
+        def spread_gates():
+            gate_rows = raw_tile([P, P])
+            nc.gpsimd.memset(gate_rows[:], 0.0)
+            nc.sync.dma_start(
+                out=gate_rows[0 : 2 * BLOCKS, :], in_=gate[:, 0, :].rearrange("r (b n) -> r b n", n=P)
+            )
+            turned = aux_bank([P, P])
+            nc.tensor.transpose(turned[:], gate_rows[:], ident[:])
+            nc.scalar.copy(out=gate_cols[:], in_=turned[:, 0 : 2 * BLOCKS])
             for r in range(2):
-                tile = raw_tile([P, T])
-                nc.sync.dma_start(out=tile[:], in_=gate[r])
-                gate_sb.append(tile)
+                for b0, nb in ((0, 4), (4, 1)):
+                    spread = aux_bank([P, nb * P])
+                    for b in range(nb):
+                        q = r * BLOCKS + b0 + b
+                        column = gate_cols[:, q : q + 1].to_broadcast([P, P])
+                        nc.tensor.transpose(spread[:, b * P : (b + 1) * P], column, ident[:])
+                    nc.scalar.copy(out=gate_sb[r][:, b0 * P : (b0 + nb) * P], in_=spread[:])
 
-        def make_slopes(c0, planes):
-            a_sb = []
-            for c in range(c0, c0 + planes):
-                tile = raw_tile([P, T])
-                nc.sync.dma_start(out=tile[:], in_=a[c * P : (c + 1) * P, :])
-                a_sb.append(tile)
-            for b in range(T // P):
-                turned = psum.tile([P, BANK], F32, name="acc", bufs=4)
-                for c in range(planes):
-                    nc.tensor.transpose(turned[:, c * P : (c + 1) * P], a_sb[c][:, b * P : (b + 1) * P], ident[:])
-                nc.scalar.activation(
-                    out=slope[b][:, c0 * P : (c0 + planes) * P], in_=turned[:, 0 : planes * P], func=RELU, scale=2.0
-                )
+        def make_slopes(b0, nb):
+            a_sb = raw_tile([P, PLANES, nb * P])
+            nc.sync.dma_start(
+                out=a_sb[:], in_=a.rearrange("(c p) n -> p c n", p=P)[:, :, b0 * P : (b0 + nb) * P]
+            )
+            for b in range(nb):
+                turned = aux_bank([P, BANK])
+                for c in range(PLANES):
+                    nc.tensor.transpose(turned[:, c * P : (c + 1) * P], a_sb[:, c, b * P : (b + 1) * P], ident[:])
+                nc.scalar.activation(out=slope[b0 + b][:], in_=turned[:], func=RELU, scale=2.0)
+
+        parts = {}
 
         def fetch(c, b0, nb):
-            parts = []
             for r in range(2):
-                part = ring.tile([P, nb * P], F32, name="part", bufs=6)
+                part = keep.tile([P, nb * P], F32, name="part%d%d%d" % (c, r, b0))
                 offsets = pos_sb[r][:, b0 * P // LIST_COL : (b0 + nb) * P // LIST_COL]
                 nc.vector.tensor_tensor(
                     out=part[:], in0=y_sb[c][:].indirect(offsets), in1=gate_sb[r][:, b0 * P : (b0 + nb) * P], op=MULT
                 )
-                parts.append(part)
-            return parts
-
-        def combine(k, c0, planes):
-            b0, nb = CHUNKS[k]
-            turned = [psum.tile([P, BANK], F32, name="turned", bufs=2) for b in range(nb)]
-            for c in range(planes):
-                parts = fetch(c0 + c, b0, nb)
                 for b in range(nb):
+                    parts[c, r, b0 + b] = part[:, b * P : (b + 1) * P]
+
+        def combine(k):
+            b0, nb = CHUNKS[k]
+            for c in range(HALF, PLANES):
+                fetch(c, b0, nb)
+            for b in range(nb):
+                if k < len(CHUNKS) - 1:
+                    turned = psum.tile([P, BANK], F32, name="acc", bufs=4)
+                else:
+                    turned = aux_bank([P, BANK])
+                for c in reversed(range(PLANES)):
                     for r in range(2):
                         nc.tensor.matmul(
-                            turned[b][:, c * P : (c + 1) * P],
-                            lhsT=parts[r][:, b * P : (b + 1) * P],
+                            turned[:, c * P : (c + 1) * P],
+                            lhsT=parts[c, r, b0 + b],
                             rhs=ident[:],
                             start=(r == 0),
                             stop=(r == 1),
                             is_transpose=True,
                         )
-            for b in range(nb):
-                cols = slice(c0 * P, (c0 + planes) * P)
-                nc.vector.tensor_tensor(
-                    out=da_rows[k][:, b, cols], in0=turned[b][:, 0 : planes * P], in1=slope[b0 + b][:, cols], op=MULT
-                )
+                nc.vector.tensor_tensor(out=da_rows[k][:, b, :], in0=turned[:], in1=slope[b0 + b][:], op=MULT)
 
         def quantize_w1():
             raw = raw_tile([P, PACK, K])
-            nc.sync.dma_start(out=raw[:], in_=w1t.rearrange("(p j) k -> p j k", j=PACK))
-            grouped = ring.tile([P, K * PACK], BF16, name="grouped", bufs=5, align_bytes=64)
+            nc.sync.dma_start(out=raw[:].rearrange("p j k -> p (j k)"), in_=w1t.rearrange("(p j) k -> p (j k)", j=PACK))
+            grouped = ring.tile([P, K * PACK], BF16, name="grouped", bufs=6, align_bytes=64)
             nc.scalar.copy(
                 out=grouped[:].rearrange("p (t m j) -> p m j t", t=PACK, j=PACK),
                 in_=raw[:].rearrange("p j (m t) -> p m j t", t=PACK),
@@ -205,7 +226,7 @@ def tile_moe_sub_relu2_kernel(
             b0, nb = CHUNKS[k]
             width = nb * P
             cols = slice(b0 * P, b0 * P + width)
-            back = psum.tile([P, 2, 2, P], F32, name="back", bufs=2)
+            back = aux_bank([P, 2, 2, P])
             words = da_rows[k][:].bitcast(F32)
             for b in range(nb):
                 for u in range(2):
@@ -221,7 +242,8 @@ def tile_moe_sub_relu2_kernel(
             result = ring.tile([P, PACK, width], F32, name="result", bufs=3, align_bytes=64)
             rounded = ring.tile([P, width, PACK], BF16, name="rounded", bufs=3, align_bytes=64)
             for b in range(nb):
-                bank = psum.tile([P, PACK, P], F32, name="acc", bufs=4)
+                last = k == len(CHUNKS) - 1
+                bank = aux_bank([P, PACK, P]) if last else psum.tile([P, PACK, P], F32, name="acc", bufs=4)
                 for t in range(PACK):
                     nc.tensor.matmul_mx(
                         out=bank[:, t, :],
@@ -232,9 +254,14 @@ def tile_moe_sub_relu2_kernel(
                         start=True,
                         stop=True,
                     )
-                copy = nc.vector.tensor_copy if k == len(CHUNKS) - 1 else nc.scalar.copy
-                copy(out=rounded[:, b * P : (b + 1) * P, :], in_=bank[:].rearrange("p t n -> p n t"))
+                if last:
+                    nc.vector.tensor_copy(out=rounded[:], in_=bank[:].rearrange("p t n -> p n t"))
                 nc.scalar.copy(out=result[:, :, b * P : (b + 1) * P], in_=bank[:])
+            if not last:
+                nc.vector.tensor_copy(
+                    out=rounded[:].rearrange("p (c i) t -> p c t i", i=4),
+                    in_=result[:].rearrange("p t (c i) -> p c t i", i=4),
+                )
             nc.vector.quantize_mx(
                 out=out_codes[:, cols].bitcast(FP8X4),
                 scales=out_scales[:, cols],
@@ -262,26 +289,23 @@ def tile_moe_sub_relu2_kernel(
         load_w2(first[0, 2][:], 0, 2, 0, PLANES)
         make_identity(nc, ident[:])
 
-        expert_group(0, 4, 0, PLANES, first)
+        expert_group(0, 3, 0, PLANES, first)
         nc.sync.dma_start(pos_sb[0][:], pos1)
         nc.sync.dma_start(pos_sb[1][:], pos2)
-        expert_group(4, 8, 0, PLANES, {})
-        c0 = 0
-        if LATE:
-            load_gates()
-            make_slopes(0, 2)
-            expert_group(8, 10, 0, 2, {})
-            for k in range(len(CHUNKS)):
-                combine(k, 0, 2)
-            c0 = 2
-        expert_group(8, 9, c0, PLANES - c0, {})
-        expert_group(9, 10, c0, PLANES - c0, {})
-        if not LATE:
-            load_gates()
-        make_slopes(c0, PLANES - c0)
+        spread_gates()
+        expert_group(3, 7, 0, PLANES, {})
+        expert_group(7, WHOLE_EXPERTS, 0, PLANES, {})
+        for e in range(WHOLE_EXPERTS, E):
+            expert_group(e, e + 1, 0, HALF, {})
+        for c in range(HALF):
+            fetch(c, 0, BLOCKS)
+        expert_group(WHOLE_EXPERTS, E, HALF, HALF, {})
+        make_slopes(0, 2)
         quantize_w1()
+        make_slopes(2, 3)
         for k in range(len(CHUNKS)):
-            combine(k, c0, PLANES - c0)
+            combine(k)
+        for k in range(len(CHUNKS)):
             finish(k)
         for q in range(4):
             queue = nc.sync if q % 2 == 0 else nc.scalar

@@ -123,6 +123,8 @@ def tile_moe_sub_relu2_kernel(
                         load_w2(raw[:], e, s, c0, planes)
                     g = e * C // GATHER
                     lodging = "slots%d" % (g + 1) if c0 == 0 and e % 2 == 1 and s == 0 and e < E - 1 else None
+                    if (e, s, c0) == (E - 1, PASSES - 1, HALF):
+                        lodging = "held_part"
                     grouped, codes, scales = mx_tiles(width, lodging)
                     if (e, s) == (E - 1, PASSES - 1):
                         for c in range(planes):
@@ -132,10 +134,10 @@ def tile_moe_sub_relu2_kernel(
                                 grouped[:, c * K_PASS : (c + 1) * K_PASS],
                                 codes[:, cols],
                                 scales[:, cols],
-                                c == 0,
+                                c0 + c == 0,
                             )
                             multiply(e, s, accs[c][:, slots], codes[:, cols], scales[:, cols])
-                            copy = nc.vector.tensor_copy if c == 0 else nc.scalar.copy
+                            copy = nc.vector.tensor_copy if c0 + c == 0 else nc.scalar.copy
                             copy(out=y_sb[c0 + c][:, e0 * C : e1 * C], in_=accs[c][:, 0 : (e1 - e0) * C])
                         return
                     round_and_quantize(raw[:], grouped[:], codes[:], scales[:], c0 == 0 and (PASSES * e + s) % 2 == 0)
@@ -177,13 +179,19 @@ def tile_moe_sub_relu2_kernel(
                 turned = aux_bank([P, BANK])
                 for c in range(PLANES):
                     nc.tensor.transpose(turned[:, c * P : (c + 1) * P], a_sb[:, c, b * P : (b + 1) * P], ident[:])
-                nc.scalar.activation(out=slope[b0 + b][:], in_=turned[:], func=RELU, scale=2.0)
+                nc.scalar.activation(
+                    out=slope[b0 + b][:].rearrange("p (u m e) -> p u m e", u=2, e=2),
+                    in_=turned[:].rearrange("p (m u e) -> p u m e", u=2, e=2),
+                    func=RELU,
+                    scale=2.0,
+                )
 
         parts = {}
 
-        def fetch(c, b0, nb):
-            for r in range(2):
-                part = keep.tile([P, nb * P], F32, name="part%d%d%d" % (c, r, b0))
+        def fetch(c, lists, b0, nb):
+            for r in lists:
+                tag = "held_part" if (c, r) == (HALF - 1, 1) else "part%d%d%d" % (c, r, b0)
+                part = keep.tile([P, nb * P], F32, name="part", tag=tag, align_bytes=64)
                 offsets = pos_sb[r][:, b0 * P // LIST_COL : (b0 + nb) * P // LIST_COL]
                 nc.vector.tensor_tensor(
                     out=part[:], in0=y_sb[c][:].indirect(offsets), in1=gate_sb[r][:, b0 * P : (b0 + nb) * P], op=MULT
@@ -194,13 +202,13 @@ def tile_moe_sub_relu2_kernel(
         def combine(k):
             b0, nb = CHUNKS[k]
             for c in range(HALF, PLANES):
-                fetch(c, b0, nb)
+                fetch(c, (0, 1), b0, nb)
             for b in range(nb):
                 if k < len(CHUNKS) - 1:
                     turned = psum.tile([P, BANK], F32, name="acc", bufs=4)
                 else:
                     turned = aux_bank([P, BANK])
-                for c in reversed(range(PLANES)):
+                for c in (2, 0, 1, 3):
                     for r in range(2):
                         nc.tensor.matmul(
                             turned[:, c * P : (c + 1) * P],
@@ -210,7 +218,12 @@ def tile_moe_sub_relu2_kernel(
                             stop=(r == 1),
                             is_transpose=True,
                         )
-                nc.vector.tensor_tensor(out=da_rows[k][:, b, :], in0=turned[:], in1=slope[b0 + b][:], op=MULT)
+                nc.vector.tensor_tensor(
+                    out=da_rows[k][:, b, :].rearrange("p (u m e) -> p u m e", u=2, e=2),
+                    in0=turned[:].rearrange("p (m u e) -> p u m e", u=2, e=2),
+                    in1=slope[b0 + b][:].rearrange("p (u m e) -> p u m e", u=2, e=2),
+                    op=MULT,
+                )
 
         def quantize_w1():
             raw = raw_tile([P, PACK, K])
@@ -230,7 +243,7 @@ def tile_moe_sub_relu2_kernel(
             words = da_rows[k][:].bitcast(F32)
             for b in range(nb):
                 for u in range(2):
-                    nc.tensor.transpose(back[:, b, u, :], words[:, b, u : H // 2 : 2], ident[:])
+                    nc.tensor.transpose(back[:, b, u, :], words[:, b, u * P : (u + 1) * P], ident[:])
             da_grouped = ring.tile([P, width * PACK], BF16, name="da_grouped", bufs=3, align_bytes=64)
             nc.scalar.copy(
                 out=da_grouped[:].bitcast(F32).rearrange("p (b n u) -> p b n u", b=nb, u=2),
@@ -297,9 +310,10 @@ def tile_moe_sub_relu2_kernel(
         expert_group(7, WHOLE_EXPERTS, 0, PLANES, {})
         for e in range(WHOLE_EXPERTS, E):
             expert_group(e, e + 1, 0, HALF, {})
-        for c in range(HALF):
-            fetch(c, 0, BLOCKS)
+        fetch(0, (0, 1), 0, BLOCKS)
+        fetch(1, (0,), 0, BLOCKS)
         expert_group(WHOLE_EXPERTS, E, HALF, HALF, {})
+        fetch(1, (1,), 0, BLOCKS)
         make_slopes(0, 2)
         quantize_w1()
         make_slopes(2, 3)

@@ -14,21 +14,26 @@ U16 = mybir.dt.uint16
 U8 = mybir.dt.uint8
 FP8X4 = mybir.dt.float8_e4m3fn_x4
 MULT = mybir.AluOpType.mult
-RELU = mybir.ActivationFunctionType.Relu
+ADD = mybir.AluOpType.add
+MAX = mybir.AluOpType.max
+COPY = mybir.ActivationFunctionType.Copy
 
 P = 128
 PACK = 4
 K_PASS = P * PACK
 PASSES = N // K_PASS
 PLANES = H // P
+HALF = PLANES // 2
 SLOTS = E * C
 LIST_COL = 16
 GATHER = 2 * C
 CHUNKS = ((0, 2), (2, 2), (4, 1))
 BLOCKS = T // P
-HALF = PLANES // 2
-WHOLE_EXPERTS = 8
+GROUPS = ((0, 3), (3, 7), (7, 8))
 BANK = 512
+TOKEN_BANK0 = 2
+BACK_BANKS = (7, 0, 1, 7, 0)
+OUT_BANKS = ((2, 3), (4, 5), (6,))
 
 
 def tile_moe_sub_relu2_kernel(
@@ -48,25 +53,25 @@ def tile_moe_sub_relu2_kernel(
         y_sb = [keep.tile([P, SLOTS], F32, name="y_sb%d" % c, align_bytes=64) for c in range(PLANES)]
         gate_cols = keep.tile([P, 2 * BLOCKS], F32, name="gate_cols")
         gate_sb = [keep.tile([P, T], F32, name="gate_sb%d" % r) for r in range(2)]
-        slope = [keep.tile([P, H], F32, name="slope%d" % b) for b in range(T // P)]
-        da_rows = [keep.tile([P, nb, H], BF16, name="da_rows%d" % b0, align_bytes=64) for b0, nb in CHUNKS]
+        dh_rows = [keep.tile([P, PACK, P], F32, name="dh_rows%d" % b, align_bytes=64) for b in range(BLOCKS)]
         w1_codes = keep.tile([P, K], U32, name="w1_codes", align_bytes=64)
         w1_scales = keep.tile([P, K], U8, name="w1_scales", align_bytes=64)
         out_codes = keep.tile([P, T], I32, name="out_codes", align_bytes=64)
         out_scales = keep.tile([P, T], U8, name="out_scales", align_bytes=64)
 
-        def raw_tile(shape):
-            return ring.tile(shape, F32, name="raw", bufs=8, align_bytes=64)
+        def bank(i, shape):
+            return psum.tile(shape, F32, name="bank", tag="bank%d" % i)
 
-        def load_w2(raw, e, s, c0, planes):
-            rows = w2t[e, s * K_PASS : (s + 1) * K_PASS, :]
+        def load_rows(rows, c0, planes):
+            raw = ring.tile([P, PACK, planes * P], F32, name="raw", bufs=8, align_bytes=64)
             if planes == PLANES:
                 nc.sync.dma_start(
-                    out=raw.rearrange("p j h -> p (j h)"), in_=rows.rearrange("(p j) h -> p (j h)", j=PACK)
+                    out=raw[:].rearrange("p j h -> p (j h)"), in_=rows.rearrange("(p j) h -> p (j h)", j=PACK)
                 )
             else:
                 rows = rows.rearrange("(p j) h -> p j h", j=PACK)
-                nc.sync.dma_start(out=raw, in_=rows[:, :, c0 * P : (c0 + planes) * P])
+                nc.sync.dma_start(out=raw[:], in_=rows[:, :, c0 * P : (c0 + planes) * P])
+            return raw
 
         def mx_tiles(words, lodging):
             if lodging is None:
@@ -77,14 +82,8 @@ def tile_moe_sub_relu2_kernel(
             scales = ring.tile([P, words], U8, name="scales", bufs=7, align_bytes=64)
             return grouped, codes, scales
 
-        def round_and_quantize(raw, grouped, codes, scales, on_vector):
-            dst = grouped.rearrange("p (c i j) -> p c j i", i=4, j=PACK)
-            src = raw.rearrange("p j (c i) -> p c j i", i=4)
-            if on_vector:
-                nc.vector.tensor_copy(out=dst, in_=src)
-            else:
-                nc.scalar.copy(out=dst, in_=src)
-            nc.vector.quantize_mx(out=codes.bitcast(FP8X4), scales=scales, in_=grouped)
+        def round_rows(copy, raw, grouped):
+            copy(out=grouped.rearrange("p (c i j) -> p c j i", i=4, j=PACK), in_=raw.rearrange("p j (c i) -> p c j i", i=4))
 
         gathered = {}
 
@@ -110,37 +109,35 @@ def tile_moe_sub_relu2_kernel(
                 stop=(s == PASSES - 1),
             )
 
-        def expert_group(e0, e1, c0, planes, preloaded):
-            width = planes * P
-            accs = [psum.tile([P, BANK], F32, name="acc", bufs=4) for c in range(planes)]
+        def expert_group(e0, e1, c0, planes, bank0, preloaded):
+            accs = [bank(bank0 + c, [P, BANK]) for c in range(planes)]
             for e in range(e0, e1):
                 slots = slice((e - e0) * C, (e - e0 + 1) * C)
                 for s in range(PASSES):
                     if (e, s) in preloaded:
                         raw = preloaded[e, s]
                     else:
-                        raw = raw_tile([P, PACK, width])
-                        load_w2(raw[:], e, s, c0, planes)
+                        raw = load_rows(w2t[e, s * K_PASS : (s + 1) * K_PASS, :], c0, planes)
                     g = e * C // GATHER
                     lodging = "slots%d" % (g + 1) if c0 == 0 and e % 2 == 1 and s == 0 and e < E - 1 else None
                     if (e, s, c0) == (E - 1, PASSES - 1, HALF):
-                        lodging = "held_part"
-                    grouped, codes, scales = mx_tiles(width, lodging)
+                        lodging = "part11"
+                    grouped, codes, scales = mx_tiles(planes * P, lodging)
                     if (e, s) == (E - 1, PASSES - 1):
                         for c in range(planes):
                             cols = slice(c * P, (c + 1) * P)
-                            round_and_quantize(
-                                raw[:, :, cols],
-                                grouped[:, c * K_PASS : (c + 1) * K_PASS],
-                                codes[:, cols],
-                                scales[:, cols],
-                                c0 + c == 0,
+                            words = slice(c * K_PASS, (c + 1) * K_PASS)
+                            copy = nc.vector.tensor_copy if c0 + c == 0 else nc.scalar.copy
+                            round_rows(copy, raw[:, :, cols], grouped[:, words])
+                            nc.vector.quantize_mx(
+                                out=codes[:, cols].bitcast(FP8X4), scales=scales[:, cols], in_=grouped[:, words]
                             )
                             multiply(e, s, accs[c][:, slots], codes[:, cols], scales[:, cols])
-                            copy = nc.vector.tensor_copy if c0 + c == 0 else nc.scalar.copy
                             copy(out=y_sb[c0 + c][:, e0 * C : e1 * C], in_=accs[c][:, 0 : (e1 - e0) * C])
                         return
-                    round_and_quantize(raw[:], grouped[:], codes[:], scales[:], c0 == 0 and (PASSES * e + s) % 2 == 0)
+                    copy = nc.vector.tensor_copy if c0 == 0 and (PASSES * e + s) % 2 == 0 else nc.scalar.copy
+                    round_rows(copy, raw[:], grouped[:])
+                    nc.vector.quantize_mx(out=codes[:].bitcast(FP8X4), scales=scales[:], in_=grouped[:])
                     if g not in gathered:
                         gather_dy(g)
                     for c in range(planes):
@@ -149,148 +146,145 @@ def tile_moe_sub_relu2_kernel(
             for c in range(planes):
                 nc.scalar.copy(out=y_sb[c0 + c][:, e0 * C : e1 * C], in_=accs[c][:, 0 : (e1 - e0) * C])
 
-        def aux_bank(shape):
-            return psum.tile(shape, F32, name="aux", bufs=4)
-
         def spread_gates():
-            gate_rows = raw_tile([P, P])
+            gate_rows = keep.tile([P, P], F32, name="gate_rows")
             nc.gpsimd.memset(gate_rows[:], 0.0)
             nc.sync.dma_start(
                 out=gate_rows[0 : 2 * BLOCKS, :], in_=gate[:, 0, :].rearrange("r (b n) -> r b n", n=P)
             )
-            turned = aux_bank([P, P])
+            turned = bank(4, [P, P])
             nc.tensor.transpose(turned[:], gate_rows[:], ident[:])
-            nc.scalar.copy(out=gate_cols[:], in_=turned[:, 0 : 2 * BLOCKS])
+            nc.scalar.activation(out=gate_cols[:], in_=turned[:, 0 : 2 * BLOCKS], func=COPY, scale=2.0)
             for r in range(2):
                 for b0, nb in ((0, 4), (4, 1)):
-                    spread = aux_bank([P, nb * P])
+                    spread = bank(5 + r + b0 // 4, [P, nb * P])
                     for b in range(nb):
                         q = r * BLOCKS + b0 + b
                         column = gate_cols[:, q : q + 1].to_broadcast([P, P])
                         nc.tensor.transpose(spread[:, b * P : (b + 1) * P], column, ident[:])
                     nc.scalar.copy(out=gate_sb[r][:, b0 * P : (b0 + nb) * P], in_=spread[:])
 
-        def make_slopes(b0, nb):
-            a_sb = raw_tile([P, PLANES, nb * P])
-            nc.sync.dma_start(
-                out=a_sb[:], in_=a.rearrange("(c p) n -> p c n", p=P)[:, :, b0 * P : (b0 + nb) * P]
-            )
-            for b in range(nb):
-                turned = aux_bank([P, BANK])
-                for c in range(PLANES):
-                    nc.tensor.transpose(turned[:, c * P : (c + 1) * P], a_sb[:, c, b * P : (b + 1) * P], ident[:])
-                nc.scalar.activation(
-                    out=slope[b0 + b][:].rearrange("p (u m e) -> p u m e", u=2, e=2),
-                    in_=turned[:].rearrange("p (m u e) -> p u m e", u=2, e=2),
-                    func=RELU,
-                    scale=2.0,
-                )
-
         parts = {}
 
-        def fetch(c, lists, b0, nb):
-            for r in lists:
-                tag = "held_part" if (c, r) == (HALF - 1, 1) else "part%d%d%d" % (c, r, b0)
-                part = keep.tile([P, nb * P], F32, name="part", tag=tag, align_bytes=64)
-                offsets = pos_sb[r][:, b0 * P // LIST_COL : (b0 + nb) * P // LIST_COL]
-                nc.vector.tensor_tensor(
-                    out=part[:], in0=y_sb[c][:].indirect(offsets), in1=gate_sb[r][:, b0 * P : (b0 + nb) * P], op=MULT
-                )
+        def window(c, r, b0, nb):
+            return y_sb[c][:].indirect(pos_sb[r][:, b0 * P // LIST_COL : (b0 + nb) * P // LIST_COL])
+
+        def note_parts(part, c0, r, b0, nb):
+            for c in range(part.shape[1]):
                 for b in range(nb):
-                    parts[c, r, b0 + b] = part[:, b * P : (b + 1) * P]
+                    parts[c0 + c, r, b0 + b] = part[:, c, b * P : (b + 1) * P]
 
-        def combine(k):
-            b0, nb = CHUNKS[k]
-            for c in range(HALF, PLANES):
-                fetch(c, (0, 1), b0, nb)
-            for b in range(nb):
-                if k < len(CHUNKS) - 1:
-                    turned = psum.tile([P, BANK], F32, name="acc", bufs=4)
-                else:
-                    turned = aux_bank([P, BANK])
-                for c in (2, 0, 1, 3):
-                    for r in range(2):
-                        nc.tensor.matmul(
-                            turned[:, c * P : (c + 1) * P],
-                            lhsT=parts[c, r, b0 + b],
-                            rhs=ident[:],
-                            start=(r == 0),
-                            stop=(r == 1),
-                            is_transpose=True,
-                        )
+        def fetch_weighted(c0, planes, r, b0, nb):
+            part = keep.tile([P, planes, nb * P], F32, name="part", tag="part%d%d" % (c0 + b0, r), align_bytes=64)
+            for c in range(planes):
                 nc.vector.tensor_tensor(
-                    out=da_rows[k][:, b, :].rearrange("p (u m e) -> p u m e", u=2, e=2),
-                    in0=turned[:].rearrange("p (m u e) -> p u m e", u=2, e=2),
-                    in1=slope[b0 + b][:].rearrange("p (u m e) -> p u m e", u=2, e=2),
-                    op=MULT,
+                    out=part[:, c, :], in0=window(c0 + c, r, b0, nb), in1=gate_sb[r][:, b0 * P : (b0 + nb) * P], op=MULT
+                )
+            note_parts(part[:], c0, r, b0, nb)
+
+        def fetch_plain(r, b0, nb):
+            part = keep.tile([P, HALF, nb * P], F32, name="part", tag="part%d%d" % (HALF + b0, r), align_bytes=64)
+            for c in range(HALF):
+                nc.scalar.activation(out=part[:, c, :], in_=window(HALF + c, r, b0, nb), func=COPY)
+            note_parts(part[:], HALF, r, b0, nb)
+            return part
+
+        def weigh(part, r, b0, nb):
+            weight = gate_sb[r][:, b0 * P : (b0 + nb) * P].unsqueeze(1).to_broadcast([P, HALF, nb * P])
+            nc.vector.tensor_tensor(out=part[:], in0=part[:], in1=weight, op=MULT)
+
+        turned = {}
+
+        def turn(planes, lists, b):
+            if b not in turned:
+                turned[b] = bank(TOKEN_BANK0 + b, [P, H])
+            for c in planes:
+                for r in lists:
+                    nc.tensor.matmul(
+                        turned[b][:, c * P : (c + 1) * P],
+                        lhsT=parts[c, r, b],
+                        rhs=ident[:],
+                        start=(r == lists[0]),
+                        stop=(r == lists[1]),
+                        is_transpose=True,
+                    )
+
+        def finish_rows(b):
+            turn(range(HALF, PLANES), (1, 0), b)
+            nc.scalar.copy(out=dh_rows[b][:], in_=turned[b][:].rearrange("p (m t) -> p t m", t=PACK))
+
+        da_grouped = [
+            keep.tile([P, nb * P, PACK], BF16, name="da_grouped", tag="bf16_chunk%d" % b0, align_bytes=64) for b0, nb in CHUNKS
+        ]
+        da_codes = keep.tile([P, T], U32, name="da_codes", align_bytes=64)
+        da_scales = keep.tile([P, T], U8, name="da_scales", align_bytes=64)
+        results = [keep.tile([P, PACK, nb * P], F32, name="result%d" % b0, align_bytes=64) for b0, nb in CHUNKS]
+        rounded = [keep.tile([P, nb * P, PACK], BF16, name="rounded", tag="bf16_chunk%d" % b0, align_bytes=64) for b0, nb in CHUNKS]
+
+        def columns(k):
+            b0, nb = CHUNKS[k]
+            return slice(b0 * P, (b0 + nb) * P)
+
+        def make_da(k, a_sb):
+            b0, nb = CHUNKS[k]
+            for b in range(b0, b0 + nb):
+                back = bank(BACK_BANKS[b], [P, PACK, P])
+                for t in range(PACK):
+                    nc.tensor.transpose(back[:, t, :], dh_rows[b][:, t, :], ident[:])
+                nc.vector.scalar_tensor_tensor(
+                    out=da_grouped[k][:, (b - b0) * P : (b - b0 + 1) * P, :],
+                    in0=a_sb[:, :, b * P : (b + 1) * P].rearrange("p t n -> p n t"),
+                    scalar=0.0,
+                    in1=back[:].rearrange("p t n -> p n t"),
+                    op0=MAX,
+                    op1=MULT,
                 )
 
-        def quantize_w1():
-            raw = raw_tile([P, PACK, K])
-            nc.sync.dma_start(out=raw[:].rearrange("p j k -> p (j k)"), in_=w1t.rearrange("(p j) k -> p (j k)", j=PACK))
-            grouped = ring.tile([P, K * PACK], BF16, name="grouped", bufs=6, align_bytes=64)
-            nc.scalar.copy(
-                out=grouped[:].rearrange("p (t m j) -> p m j t", t=PACK, j=PACK),
-                in_=raw[:].rearrange("p j (m t) -> p m j t", t=PACK),
+        def quantize_da(k):
+            nc.vector.quantize_mx(
+                out=da_codes[:, columns(k)].bitcast(FP8X4),
+                scales=da_scales[:, columns(k)],
+                in_=da_grouped[k][:].rearrange("p n t -> p (n t)"),
             )
-            nc.vector.quantize_mx(out=w1_codes[:].bitcast(FP8X4), scales=w1_scales[:], in_=grouped[:])
 
-        def finish(k):
-            b0, nb = CHUNKS[k]
-            width = nb * P
-            cols = slice(b0 * P, b0 * P + width)
-            back = aux_bank([P, 2, 2, P])
-            words = da_rows[k][:].bitcast(F32)
-            for b in range(nb):
-                for u in range(2):
-                    nc.tensor.transpose(back[:, b, u, :], words[:, b, u * P : (u + 1) * P], ident[:])
-            da_grouped = ring.tile([P, width * PACK], BF16, name="da_grouped", bufs=3, align_bytes=64)
-            nc.scalar.copy(
-                out=da_grouped[:].bitcast(F32).rearrange("p (b n u) -> p b n u", b=nb, u=2),
-                in_=back[:, 0:nb, :, :].rearrange("p b u n -> p b n u"),
-            )
-            da_codes = ring.tile([P, width], U32, name="da_codes", bufs=3, align_bytes=64)
-            da_scales = ring.tile([P, width], U8, name="da_scales", bufs=3, align_bytes=64)
-            nc.vector.quantize_mx(out=da_codes[:].bitcast(FP8X4), scales=da_scales[:], in_=da_grouped[:])
-            result = ring.tile([P, PACK, width], F32, name="result", bufs=3, align_bytes=64)
-            rounded = ring.tile([P, width, PACK], BF16, name="rounded", bufs=3, align_bytes=64)
-            for b in range(nb):
-                last = k == len(CHUNKS) - 1
-                bank = aux_bank([P, PACK, P]) if last else psum.tile([P, PACK, P], F32, name="acc", bufs=4)
-                for t in range(PACK):
+        def project(k):
+            width = CHUNKS[k][1] * P
+            per_bank = BANK // width
+            for t0 in range(0, PACK, per_bank):
+                acc = bank(OUT_BANKS[k][t0 // per_bank], [P, per_bank, width])
+                for t in range(t0, t0 + per_bank):
                     nc.tensor.matmul_mx(
-                        out=bank[:, t, :],
+                        out=acc[:, t - t0, :],
                         lhsT=w1_codes[:, t * P : (t + 1) * P].bitcast(FP8X4),
                         lhsT_scale=w1_scales[:, t * P : (t + 1) * P],
-                        rhs=da_codes[:, b * P : (b + 1) * P].bitcast(FP8X4),
-                        rhs_scale=da_scales[:, b * P : (b + 1) * P],
+                        rhs=da_codes[:, columns(k)].bitcast(FP8X4),
+                        rhs_scale=da_scales[:, columns(k)],
                         start=True,
                         stop=True,
                     )
-                if last:
-                    nc.vector.tensor_copy(out=rounded[:], in_=bank[:].rearrange("p t n -> p n t"))
-                nc.scalar.copy(out=result[:, :, b * P : (b + 1) * P], in_=bank[:])
-            if not last:
-                nc.vector.tensor_copy(
-                    out=rounded[:].rearrange("p (c i) t -> p c t i", i=4),
-                    in_=result[:].rearrange("p t (c i) -> p c t i", i=4),
-                )
-            nc.vector.quantize_mx(
-                out=out_codes[:, cols].bitcast(FP8X4),
-                scales=out_scales[:, cols],
-                in_=rounded[:].rearrange("p n t -> p (n t)"),
+                nc.scalar.copy(out=results[k][:, t0 : t0 + per_bank, :], in_=acc[:])
+            nc.sync.dma_start(out=out_0.rearrange("(p t) n -> p t n", t=PACK)[:, :, columns(k)], in_=results[k][:])
+
+        def round_result(k):
+            nc.vector.tensor_copy(
+                out=rounded[k][:].rearrange("p (c i) t -> p c t i", i=4),
+                in_=results[k][:].rearrange("p t (c i) -> p c t i", i=4),
             )
-            nc.sync.dma_start(out=out_0.rearrange("(p t) n -> p t n", t=PACK)[:, :, cols], in_=result[:])
+
+        def quantize_result(k):
+            nc.vector.quantize_mx(
+                out=out_codes[:, columns(k)].bitcast(FP8X4),
+                scales=out_scales[:, columns(k)],
+                in_=rounded[k][:].rearrange("p n t -> p (n t)"),
+            )
             nc.sync.dma_start(
-                out=out_1[0].rearrange("p n d -> p (n d)").bitcast(I32)[:, cols], in_=out_codes[:, cols]
+                out=out_1[0].rearrange("p n d -> p (n d)").bitcast(I32)[:, columns(k)], in_=out_codes[:, columns(k)]
             )
 
         nc.sync.dma_start(offs_sb[:], offs)
         first = {}
-        for s in range(PASSES):
-            first[0, s] = raw_tile([P, PACK, H])
-            if s < 2:
-                load_w2(first[0, s][:], 0, s, 0, PLANES)
+        for s in range(2):
+            first[0, s] = load_rows(w2t[0, s * K_PASS : (s + 1) * K_PASS, :], 0, PLANES)
         for s in range(PASSES):
             nc.sync.dma_start(out=dy_word_sb[s][:], in_=dy_words[s].rearrange("p n d -> p (n d)").bitcast(I32))
         nc.gpsimd.memset(dy_scale_sb[:].bitcast(I32), 0)
@@ -299,28 +293,55 @@ def tile_moe_sub_relu2_kernel(
                 out=dy_scale_sb[32 * q : 32 * q + 4 * PASSES, :].bitcast(I32),
                 in_=dy_scales[:, 4 * q : 4 * q + 4, :].bitcast(I32),
             )
-        load_w2(first[0, 2][:], 0, 2, 0, PLANES)
         make_identity(nc, ident[:])
 
-        expert_group(0, 3, 0, PLANES, first)
+        expert_group(*GROUPS[0], 0, PLANES, 0, first)
         nc.sync.dma_start(pos_sb[0][:], pos1)
         nc.sync.dma_start(pos_sb[1][:], pos2)
         spread_gates()
-        expert_group(3, 7, 0, PLANES, {})
-        expert_group(7, WHOLE_EXPERTS, 0, PLANES, {})
-        for e in range(WHOLE_EXPERTS, E):
-            expert_group(e, e + 1, 0, HALF, {})
-        fetch(0, (0, 1), 0, BLOCKS)
-        fetch(1, (0,), 0, BLOCKS)
-        expert_group(WHOLE_EXPERTS, E, HALF, HALF, {})
-        fetch(1, (1,), 0, BLOCKS)
-        make_slopes(0, 2)
-        quantize_w1()
-        make_slopes(2, 3)
+        expert_group(*GROUPS[1], 0, PLANES, 4, {})
+        expert_group(*GROUPS[2], 0, PLANES, 0, {})
+        expert_group(E - 2, E - 1, 0, HALF, 4, {})
+        expert_group(E - 1, E, 0, HALF, 6, {})
+        expert_group(E - 2, E, HALF, HALF, 0, {})
+        w1_raw = load_rows(w1t, 0, PLANES)
+        a_sb = ring.tile([P, PACK, T], F32, name="raw", bufs=8, align_bytes=64)
+        nc.sync.dma_start(out=a_sb[:].rearrange("p t n -> p (t n)"), in_=a.rearrange("(p t) n -> p (t n)", t=PACK))
+
+        for c in range(HALF):
+            for r in range(2):
+                fetch_weighted(c, 1, r, 0, BLOCKS)
+            for b in range(BLOCKS):
+                turn([c], (0, 1), b)
+        plain = fetch_plain(0, *CHUNKS[0])
+        fetch_weighted(HALF, HALF, 1, *CHUNKS[0])
+        weigh(plain, 0, *CHUNKS[0])
+        plain = fetch_plain(0, *CHUNKS[1])
+        finish_rows(0)
+        finish_rows(1)
+        fetch_weighted(HALF, HALF, 1, *CHUNKS[1])
+        weigh(plain, 0, *CHUNKS[1])
+        for r in range(2):
+            fetch_weighted(HALF, HALF, r, *CHUNKS[2])
+        make_da(0, a_sb)
+        for b in range(2, BLOCKS):
+            finish_rows(b)
+        w1_grouped = ring.tile([P, K * PACK], BF16, name="grouped", bufs=6, align_bytes=64)
+        nc.scalar.copy(
+            out=w1_grouped[:].rearrange("p (t m j) -> p m j t", t=PACK, j=PACK),
+            in_=w1_raw[:].rearrange("p j (m t) -> p m j t", t=PACK),
+        )
+        quantize_da(0)
+        make_da(1, a_sb)
+        nc.vector.quantize_mx(out=w1_codes[:].bitcast(FP8X4), scales=w1_scales[:], in_=w1_grouped[:])
+        quantize_da(1)
+        make_da(2, a_sb)
+        quantize_da(2)
         for k in range(len(CHUNKS)):
-            combine(k)
+            project(k)
         for k in range(len(CHUNKS)):
-            finish(k)
+            round_result(k)
+            quantize_result(k)
         for q in range(4):
             queue = nc.sync if q % 2 == 0 else nc.scalar
             queue.dma_start(

@@ -127,12 +127,13 @@ def tile_moe_sub_relu2_kernel(
                         for c in range(planes):
                             cols = slice(c * P, (c + 1) * P)
                             words = slice(c * K_PASS, (c + 1) * K_PASS)
-                            copy = nc.vector.tensor_copy if c0 + c == 0 else nc.scalar.copy
+                            copy = nc.vector.tensor_copy if c == 0 else nc.scalar.copy
                             round_rows(copy, raw[:, :, cols], grouped[:, words])
                             nc.vector.quantize_mx(
                                 out=codes[:, cols].bitcast(FP8X4), scales=scales[:, cols], in_=grouped[:, words]
                             )
                             multiply(e, s, accs[c][:, slots], codes[:, cols], scales[:, cols])
+                            copy = nc.vector.tensor_copy if c0 + c == 0 else nc.scalar.copy
                             copy(out=y_sb[c0 + c][:, e0 * C : e1 * C], in_=accs[c][:, 0 : (e1 - e0) * C])
                         return
                     copy = nc.vector.tensor_copy if c0 == 0 and (PASSES * e + s) % 2 == 0 else nc.scalar.copy
@@ -195,22 +196,22 @@ def tile_moe_sub_relu2_kernel(
 
         turned = {}
 
-        def turn(planes, lists, b):
-            if b not in turned:
-                turned[b] = bank(TOKEN_BANK0 + b, [P, H])
-            for c in planes:
-                for r in lists:
+        def turn(planes, r, blocks):
+            for b in blocks:
+                if b not in turned:
+                    turned[b] = bank(TOKEN_BANK0 + b, [P, H])
+                for c in planes:
                     nc.tensor.matmul(
                         turned[b][:, c * P : (c + 1) * P],
                         lhsT=parts[c, r, b],
                         rhs=ident[:],
-                        start=(r == lists[0]),
-                        stop=(r == lists[1]),
+                        start=((c, r) == (0, 0)),
+                        stop=((c, r) == (PLANES - 1, 0)),
                         is_transpose=True,
                     )
 
         def finish_rows(b):
-            turn(range(HALF, PLANES), (1, 0), b)
+            turn(range(HALF, PLANES), 0, [b])
             nc.scalar.copy(out=dh_rows[b][:], in_=turned[b][:].rearrange("p (m t) -> p t m", t=PACK))
 
         da_grouped = [
@@ -311,33 +312,37 @@ def tile_moe_sub_relu2_kernel(
         for c in range(HALF):
             for r in range(2):
                 fetch_weighted(c, 1, r, 0, BLOCKS)
-            for b in range(BLOCKS):
-                turn([c], (0, 1), b)
+                turn([c], r, range(BLOCKS))
         plain = fetch_plain(0, *CHUNKS[0])
         fetch_weighted(HALF, HALF, 1, *CHUNKS[0])
+        turn(range(HALF, PLANES), 1, (0, 1))
         weigh(plain, 0, *CHUNKS[0])
         plain = fetch_plain(0, *CHUNKS[1])
+        last_plain = fetch_plain(0, *CHUNKS[2])
         finish_rows(0)
         finish_rows(1)
         fetch_weighted(HALF, HALF, 1, *CHUNKS[1])
         weigh(plain, 0, *CHUNKS[1])
-        for r in range(2):
-            fetch_weighted(HALF, HALF, r, *CHUNKS[2])
+        fetch_weighted(HALF, HALF, 1, *CHUNKS[2])
+        weigh(last_plain, 0, *CHUNKS[2])
         make_da(0, a_sb)
+        turn(range(HALF, PLANES), 1, (2, 3, 4))
+        w1_grouped = keep.tile([P, K * PACK], BF16, name="w1_grouped", tag="part20", align_bytes=64)
+        for copy, words in ((nc.scalar.copy, slice(0, P // 2)), (nc.vector.tensor_copy, slice(P // 2, P))):
+            copy(
+                out=w1_grouped[:].rearrange("p (t m j) -> p m j t", t=PACK, j=PACK)[:, words],
+                in_=w1_raw[:].rearrange("p j (m t) -> p m j t", t=PACK)[:, words],
+            )
         for b in range(2, BLOCKS):
             finish_rows(b)
-        w1_grouped = ring.tile([P, K * PACK], BF16, name="grouped", bufs=6, align_bytes=64)
-        nc.scalar.copy(
-            out=w1_grouped[:].rearrange("p (t m j) -> p m j t", t=PACK, j=PACK),
-            in_=w1_raw[:].rearrange("p j (m t) -> p m j t", t=PACK),
-        )
         quantize_da(0)
-        make_da(1, a_sb)
         nc.vector.quantize_mx(out=w1_codes[:].bitcast(FP8X4), scales=w1_scales[:], in_=w1_grouped[:])
+        make_da(1, a_sb)
+        project(0)
         quantize_da(1)
         make_da(2, a_sb)
         quantize_da(2)
-        for k in range(len(CHUNKS)):
+        for k in (1, 2):
             project(k)
         for k in range(len(CHUNKS)):
             round_result(k)

@@ -31,6 +31,11 @@ CHUNKS = ((0, 2), (2, 2), (4, 1))
 BLOCKS = T // P
 GROUPS = ((0, 3), (3, 7), (7, 8))
 BANK = 512
+WHOLE_LOADS = 6
+EXPERT_SLOTS = 3
+EXPERT_BYTES = PASSES * PACK * H * 4
+STAGE_SLOTS = 8
+SLOT_BYTES = PACK * T * 4
 TOKEN_BANK0 = 2
 BACK_BANKS = (7, 0, 1, 7, 0)
 OUT_BANKS = ((2, 3), (4, 5), (6,))
@@ -43,11 +48,12 @@ def tile_moe_sub_relu2_kernel(
     with ExitStack() as ctx:
         keep = ctx.enter_context(tc.tile_pool(name="keep", bufs=1))
         ring = ctx.enter_context(tc.tile_pool(name="ring", bufs=1))
+        stage = ctx.enter_context(tc.tile_pool(name="stage", bufs=1))
         psum = ctx.enter_context(tc.psum_pool(name="psum", bufs=1))
 
         offs_sb = keep.tile([P, SLOTS // LIST_COL], U16, name="offs_sb")
         pos_sb = [keep.tile([P, T // LIST_COL], U16, name="pos_sb%d" % r) for r in range(2)]
-        dy_word_sb = [keep.tile([P, T], I32, name="dy_word_sb%d" % s, align_bytes=64) for s in range(PASSES)]
+        dy_word_sb = keep.tile([P, PASSES, T], I32, name="dy_word_sb", align_bytes=64)
         dy_scale_sb = keep.tile([P, T], U8, name="dy_scale_sb", align_bytes=64)
         ident = keep.tile([P, P], F32, name="ident")
         y_sb = [keep.tile([P, SLOTS], F32, name="y_sb%d" % c, align_bytes=64) for c in range(PLANES)]
@@ -62,8 +68,25 @@ def tile_moe_sub_relu2_kernel(
         def bank(i, shape):
             return psum.tile(shape, F32, name="bank", tag="bank%d" % i)
 
+        staged = []
+
+        def stage_tile(shape):
+            slot = len(staged) % STAGE_SLOTS
+            staged.append(slot)
+            return stage.tile(shape, F32, name="raw", tag="raw%d" % slot, offset=slot * SLOT_BYTES, align_bytes=64)
+
+        def load_expert(e):
+            slot = e % EXPERT_SLOTS
+            raw = stage.tile(
+                [P, PASSES, PACK, H], F32, name="expert", tag="expert%d" % slot, offset=slot * EXPERT_BYTES, align_bytes=64
+            )
+            nc.sync.dma_start(
+                out=raw[:].rearrange("p s j h -> p s (j h)"), in_=w2t[e].rearrange("(s p j) h -> p s (j h)", p=P, j=PACK)
+            )
+            return {(e, s): raw[:, s] for s in range(PASSES)}
+
         def load_rows(rows, c0, planes):
-            raw = ring.tile([P, PACK, planes * P], F32, name="raw", bufs=8, align_bytes=64)
+            raw = stage_tile([P, PACK, planes * P])
             if planes == PLANES:
                 nc.sync.dma_start(
                     out=raw[:].rearrange("p j h -> p (j h)"), in_=rows.rearrange("(p j) h -> p (j h)", j=PACK)
@@ -71,7 +94,7 @@ def tile_moe_sub_relu2_kernel(
             else:
                 rows = rows.rearrange("(p j) h -> p j h", j=PACK)
                 nc.sync.dma_start(out=raw[:], in_=rows[:, :, c0 * P : (c0 + planes) * P])
-            return raw
+            return raw[:]
 
         def mx_tiles(words, lodging):
             if lodging is None:
@@ -91,7 +114,7 @@ def tile_moe_sub_relu2_kernel(
             offsets = offs_sb[:, g * GATHER // LIST_COL : (g + 1) * GATHER // LIST_COL]
             words = keep.tile([P, PASSES, GATHER], U32, name="slot_words", tag="slots%d" % g, align_bytes=64)
             for s in range(PASSES):
-                nc.vector.tensor_copy(out=words[:, s, :], in_=dy_word_sb[s][:].bitcast(U32).indirect(offsets))
+                nc.vector.tensor_copy(out=words[:, s, :], in_=dy_word_sb[:, s, :].bitcast(U32).indirect(offsets))
             z = keep.tile([P, GATHER], U8, name="slot_scales%d" % g, align_bytes=64)
             nc.vector.tensor_copy(out=z[:], in_=dy_scale_sb[:].indirect(offsets))
             gathered[g] = (words, z)
@@ -109,43 +132,49 @@ def tile_moe_sub_relu2_kernel(
                 stop=(s == PASSES - 1),
             )
 
+        def weight_pass(e, s, c0, planes, accs, on_vector, lodging=None, raw=None):
+            if raw is None:
+                raw = load_rows(w2t[e, s * K_PASS : (s + 1) * K_PASS, :], c0, planes)
+            grouped, codes, scales = mx_tiles(planes * P, lodging)
+            round_rows(nc.vector.tensor_copy if on_vector else nc.scalar.copy, raw, grouped[:])
+            nc.vector.quantize_mx(out=codes[:].bitcast(FP8X4), scales=scales[:], in_=grouped[:])
+            if e * C // GATHER not in gathered:
+                gather_dy(e * C // GATHER)
+            for c in range(planes):
+                cols = slice(c * P, (c + 1) * P)
+                multiply(e, s, accs[c], codes[:, cols], scales[:, cols])
+
+        def last_pass(c0, accs, e0, lodging):
+            raw = load_rows(w2t[E - 1, (PASSES - 1) * K_PASS :, :], c0, HALF)
+            grouped, codes, scales = mx_tiles(HALF * P, lodging)
+            for c in range(HALF):
+                cols = slice(c * P, (c + 1) * P)
+                words = slice(c * K_PASS, (c + 1) * K_PASS)
+                round_rows(nc.vector.tensor_copy if c == 0 else nc.scalar.copy, raw[:, :, cols], grouped[:, words])
+                nc.vector.quantize_mx(out=codes[:, cols].bitcast(FP8X4), scales=scales[:, cols], in_=grouped[:, words])
+                multiply(E - 1, PASSES - 1, accs[c][:, (E - 1 - e0) * C : (E - e0) * C], codes[:, cols], scales[:, cols])
+                copy = nc.vector.tensor_copy if c0 + c == 0 else nc.scalar.copy
+                copy(out=y_sb[c0 + c][:, e0 * C :], in_=accs[c][:, 0 : (E - e0) * C])
+
+        def keep_sums(accs, c0, e0, e1):
+            for c, acc in enumerate(accs):
+                nc.scalar.copy(out=y_sb[c0 + c][:, e0 * C : e1 * C], in_=acc[:, 0 : (e1 - e0) * C])
+
         def expert_group(e0, e1, c0, planes, bank0, preloaded):
             accs = [bank(bank0 + c, [P, BANK]) for c in range(planes)]
             for e in range(e0, e1):
-                slots = slice((e - e0) * C, (e - e0 + 1) * C)
+                if 0 < e < WHOLE_LOADS:
+                    preloaded = load_expert(e)
+                sums = [acc[:, (e - e0) * C : (e - e0 + 1) * C] for acc in accs]
                 for s in range(PASSES):
-                    if (e, s) in preloaded:
-                        raw = preloaded[e, s]
-                    else:
-                        raw = load_rows(w2t[e, s * K_PASS : (s + 1) * K_PASS, :], c0, planes)
+                    if (e, s) == (E - 1, PASSES - 1):
+                        last_pass(c0, accs, e0, "part11" if c0 == HALF else None)
+                        return
                     g = e * C // GATHER
                     lodging = "slots%d" % (g + 1) if c0 == 0 and e % 2 == 1 and s == 0 and e < E - 1 else None
-                    if (e, s, c0) == (E - 1, PASSES - 1, HALF):
-                        lodging = "part11"
-                    grouped, codes, scales = mx_tiles(planes * P, lodging)
-                    if (e, s) == (E - 1, PASSES - 1):
-                        for c in range(planes):
-                            cols = slice(c * P, (c + 1) * P)
-                            words = slice(c * K_PASS, (c + 1) * K_PASS)
-                            copy = nc.vector.tensor_copy if c == 0 else nc.scalar.copy
-                            round_rows(copy, raw[:, :, cols], grouped[:, words])
-                            nc.vector.quantize_mx(
-                                out=codes[:, cols].bitcast(FP8X4), scales=scales[:, cols], in_=grouped[:, words]
-                            )
-                            multiply(e, s, accs[c][:, slots], codes[:, cols], scales[:, cols])
-                            copy = nc.vector.tensor_copy if c0 + c == 0 else nc.scalar.copy
-                            copy(out=y_sb[c0 + c][:, e0 * C : e1 * C], in_=accs[c][:, 0 : (e1 - e0) * C])
-                        return
-                    copy = nc.vector.tensor_copy if c0 == 0 and (PASSES * e + s) % 2 == 0 else nc.scalar.copy
-                    round_rows(copy, raw[:], grouped[:])
-                    nc.vector.quantize_mx(out=codes[:].bitcast(FP8X4), scales=scales[:], in_=grouped[:])
-                    if g not in gathered:
-                        gather_dy(g)
-                    for c in range(planes):
-                        cols = slice(c * P, (c + 1) * P)
-                        multiply(e, s, accs[c][:, slots], codes[:, cols], scales[:, cols])
-            for c in range(planes):
-                nc.scalar.copy(out=y_sb[c0 + c][:, e0 * C : e1 * C], in_=accs[c][:, 0 : (e1 - e0) * C])
+                    on_vector = c0 == 0 and (PASSES * e + s) % 2 == 0
+                    weight_pass(e, s, c0, planes, sums, on_vector, lodging, preloaded.get((e, s)))
+            keep_sums(accs, c0, e0, e1)
 
         def spread_gates():
             gate_rows = keep.tile([P, P], F32, name="gate_rows")
@@ -282,18 +311,18 @@ def tile_moe_sub_relu2_kernel(
                 out=out_1[0].rearrange("p n d -> p (n d)").bitcast(I32)[:, columns(k)], in_=out_codes[:, columns(k)]
             )
 
-        nc.sync.dma_start(offs_sb[:], offs)
-        first = {}
-        for s in range(2):
-            first[0, s] = load_rows(w2t[0, s * K_PASS : (s + 1) * K_PASS, :], 0, PLANES)
-        for s in range(PASSES):
-            nc.sync.dma_start(out=dy_word_sb[s][:], in_=dy_words[s].rearrange("p n d -> p (n d)").bitcast(I32))
-        nc.gpsimd.memset(dy_scale_sb[:].bitcast(I32), 0)
-        for q in range(4):
+        def load_scales(q):
             nc.sync.dma_start(
                 out=dy_scale_sb[32 * q : 32 * q + 4 * PASSES, :].bitcast(I32),
                 in_=dy_scales[:, 4 * q : 4 * q + 4, :].bitcast(I32),
             )
+
+        nc.vector.memset(dy_scale_sb[:].bitcast(I32), 0)
+        first = load_expert(0)
+        nc.sync.dma_start(out=dy_word_sb[:], in_=dy_words.rearrange("s p n d -> p s (n d)").bitcast(I32))
+        nc.sync.dma_start(offs_sb[:], offs)
+        for q in range(4):
+            load_scales(q)
         make_identity(nc, ident[:])
 
         expert_group(*GROUPS[0], 0, PLANES, 0, first)
@@ -306,7 +335,7 @@ def tile_moe_sub_relu2_kernel(
         expert_group(E - 1, E, 0, HALF, 6, {})
         expert_group(E - 2, E, HALF, HALF, 0, {})
         w1_raw = load_rows(w1t, 0, PLANES)
-        a_sb = ring.tile([P, PACK, T], F32, name="raw", bufs=8, align_bytes=64)
+        a_sb = stage_tile([P, PACK, T])
         nc.sync.dma_start(out=a_sb[:].rearrange("p t n -> p (t n)"), in_=a.rearrange("(p t) n -> p (t n)", t=PACK))
 
         for c in range(HALF):
@@ -331,7 +360,7 @@ def tile_moe_sub_relu2_kernel(
         for copy, words in ((nc.scalar.copy, slice(0, P // 2)), (nc.vector.tensor_copy, slice(P // 2, P))):
             copy(
                 out=w1_grouped[:].rearrange("p (t m j) -> p m j t", t=PACK, j=PACK)[:, words],
-                in_=w1_raw[:].rearrange("p j (m t) -> p m j t", t=PACK)[:, words],
+                in_=w1_raw.rearrange("p j (m t) -> p m j t", t=PACK)[:, words],
             )
         for b in range(2, BLOCKS):
             finish_rows(b)

@@ -307,9 +307,6 @@ def tile_moe_sub_relu2_kernel(
                 scales=out_scales[:, columns(k)],
                 in_=rounded[k][:].rearrange("p n t -> p (n t)"),
             )
-            nc.sync.dma_start(
-                out=out_1[0].rearrange("p n d -> p (n d)").bitcast(I32)[:, columns(k)], in_=out_codes[:, columns(k)]
-            )
 
         def load_scales(q):
             nc.sync.dma_start(
@@ -373,9 +370,13 @@ def tile_moe_sub_relu2_kernel(
         quantize_da(2)
         for k in (1, 2):
             project(k)
+        words_out = out_1[0].rearrange("p n d -> p (n d)").bitcast(I32)
         for k in range(len(CHUNKS)):
             round_result(k)
             quantize_result(k)
+            if k > 0:
+                cols = slice(0 if k == 1 else columns(k).start, columns(k).stop)
+                nc.scalar.dma_start(out=words_out[:, cols], in_=out_codes[:, cols])
         for q in range(4):
             queue = nc.sync if q % 2 == 0 else nc.scalar
             queue.dma_start(

@@ -38,7 +38,8 @@ STAGE_SLOTS = 8
 SLOT_BYTES = PACK * T * 4
 TOKEN_BANK0 = 2
 BACK_BANKS = (7, 0, 1, 7, 0)
-OUT_BANKS = ((2, 3), (4, 5), (6,))
+PIECES = ((0, 256), (256, 256), (512, 64), (576, 64))
+OUT_BANKS = ((2, 3), (4, 5), (6,), (7,))
 
 
 def tile_moe_sub_relu2_kernel(
@@ -244,28 +245,41 @@ def tile_moe_sub_relu2_kernel(
             nc.scalar.copy(out=dh_rows[b][:], in_=turned[b][:].rearrange("p (m t) -> p t m", t=PACK))
 
         da_grouped = [
-            keep.tile([P, nb * P, PACK], BF16, name="da_grouped", tag="bf16_chunk%d" % b0, align_bytes=64) for b0, nb in CHUNKS
+            keep.tile([P, n, PACK], BF16, name="da_grouped", tag="bf16_piece%d" % n0, align_bytes=64) for n0, n in PIECES
         ]
         da_codes = keep.tile([P, T], U32, name="da_codes", align_bytes=64)
         da_scales = keep.tile([P, T], U8, name="da_scales", align_bytes=64)
         results = [keep.tile([P, PACK, nb * P], F32, name="result%d" % b0, align_bytes=64) for b0, nb in CHUNKS]
-        rounded = [keep.tile([P, nb * P, PACK], BF16, name="rounded", tag="bf16_chunk%d" % b0, align_bytes=64) for b0, nb in CHUNKS]
+        rounded = [
+            keep.tile([P, nb * P, PACK], BF16, name="rounded", tag="bf16_piece%d" % (b0 * P), align_bytes=64)
+            for b0, nb in CHUNKS
+        ]
 
         def columns(k):
-            b0, nb = CHUNKS[k]
-            return slice(b0 * P, (b0 + nb) * P)
+            n0, n = PIECES[k]
+            return slice(n0, n0 + n)
+
+        def result_of(k):
+            n0, n = PIECES[k]
+            at = n0 % (2 * P)
+            return results[n0 // (2 * P)][:, :, at : at + n]
+
+        backs = {}
 
         def make_da(k, a_sb):
-            b0, nb = CHUNKS[k]
-            for b in range(b0, b0 + nb):
-                back = bank(BACK_BANKS[b], [P, PACK, P])
-                for t in range(PACK):
-                    nc.tensor.transpose(back[:, t, :], dh_rows[b][:, t, :], ident[:])
+            n0, n = PIECES[k]
+            step = min(n, P)
+            for at in range(n0, n0 + n, step):
+                b = at // P
+                if b not in backs:
+                    backs[b] = bank(BACK_BANKS[b], [P, PACK, P])
+                    for t in range(PACK):
+                        nc.tensor.transpose(backs[b][:, t, :], dh_rows[b][:, t, :], ident[:])
                 nc.vector.scalar_tensor_tensor(
-                    out=da_grouped[k][:, (b - b0) * P : (b - b0 + 1) * P, :],
-                    in0=a_sb[:, :, b * P : (b + 1) * P].rearrange("p t n -> p n t"),
+                    out=da_grouped[k][:, at - n0 : at - n0 + step, :],
+                    in0=a_sb[:, :, at : at + step].rearrange("p t n -> p n t"),
                     scalar=0.0,
-                    in1=back[:].rearrange("p t n -> p n t"),
+                    in1=backs[b][:, :, at % P : at % P + step].rearrange("p t n -> p n t"),
                     op0=MAX,
                     op1=MULT,
                 )
@@ -278,8 +292,8 @@ def tile_moe_sub_relu2_kernel(
             )
 
         def project(k):
-            width = CHUNKS[k][1] * P
-            per_bank = BANK // width
+            width = PIECES[k][1]
+            per_bank = min(PACK, BANK // width)
             for t0 in range(0, PACK, per_bank):
                 acc = bank(OUT_BANKS[k][t0 // per_bank], [P, per_bank, width])
                 for t in range(t0, t0 + per_bank):
@@ -292,20 +306,26 @@ def tile_moe_sub_relu2_kernel(
                         start=True,
                         stop=True,
                     )
-                nc.scalar.copy(out=results[k][:, t0 : t0 + per_bank, :], in_=acc[:])
-            nc.sync.dma_start(out=out_0.rearrange("(p t) n -> p t n", t=PACK)[:, :, columns(k)], in_=results[k][:])
+                nc.scalar.copy(out=result_of(k)[:, t0 : t0 + per_bank, :], in_=acc[:])
 
-        def round_result(k):
-            nc.vector.tensor_copy(
-                out=rounded[k][:].rearrange("p (c i) t -> p c t i", i=4),
-                in_=results[k][:].rearrange("p t (c i) -> p c t i", i=4),
+        def store(chunk, rows):
+            b0, nb = CHUNKS[chunk]
+            nc.sync.dma_start(
+                out=out_0.rearrange("(p t) n -> p t n", t=PACK)[:, rows, b0 * P : (b0 + nb) * P],
+                in_=results[chunk][:, rows, :],
             )
 
-        def quantize_result(k):
+        def quantize_result(chunk):
+            b0, nb = CHUNKS[chunk]
+            cols = slice(b0 * P, (b0 + nb) * P)
+            nc.vector.tensor_copy(
+                out=rounded[chunk][:].rearrange("p (c i) t -> p c t i", i=4),
+                in_=results[chunk][:].rearrange("p t (c i) -> p c t i", i=4),
+            )
             nc.vector.quantize_mx(
-                out=out_codes[:, columns(k)].bitcast(FP8X4),
-                scales=out_scales[:, columns(k)],
-                in_=rounded[k][:].rearrange("p n t -> p (n t)"),
+                out=out_codes[:, cols].bitcast(FP8X4),
+                scales=out_scales[:, cols],
+                in_=rounded[chunk][:].rearrange("p n t -> p (n t)"),
             )
 
         def load_scales(q):
@@ -365,18 +385,24 @@ def tile_moe_sub_relu2_kernel(
         nc.vector.quantize_mx(out=w1_codes[:].bitcast(FP8X4), scales=w1_scales[:], in_=w1_grouped[:])
         make_da(1, a_sb)
         project(0)
+        store(0, slice(0, 2))
+        store(0, slice(2, PACK))
         quantize_da(1)
-        make_da(2, a_sb)
-        quantize_da(2)
-        for k in (1, 2):
-            project(k)
+        for k in (2, 3):
+            make_da(k, a_sb)
+            quantize_da(k)
+        project(1)
+        store(1, slice(0, 2))
+        store(1, slice(2, PACK))
+        project(2)
+        project(3)
+        store(2, slice(0, PACK))
         words_out = out_1[0].rearrange("p n d -> p (n d)").bitcast(I32)
-        for k in range(len(CHUNKS)):
-            round_result(k)
-            quantize_result(k)
-            if k > 0:
-                cols = slice(0 if k == 1 else columns(k).start, columns(k).stop)
-                nc.scalar.dma_start(out=words_out[:, cols], in_=out_codes[:, cols])
+        quantize_result(0)
+        quantize_result(1)
+        nc.scalar.dma_start(out=words_out[:, 0 : 4 * P], in_=out_codes[:, 0 : 4 * P])
+        quantize_result(2)
+        nc.scalar.dma_start(out=words_out[:, 4 * P :], in_=out_codes[:, 4 * P :])
         for q in range(4):
             queue = nc.sync if q % 2 == 0 else nc.scalar
             queue.dma_start(

@@ -16,6 +16,8 @@ FP8X4 = mybir.dt.float8_e4m3fn_x4
 MULT = mybir.AluOpType.mult
 ADD = mybir.AluOpType.add
 MAX = mybir.AluOpType.max
+SUBTRACT = mybir.AluOpType.subtract
+IS_LT = mybir.AluOpType.is_lt
 COPY = mybir.ActivationFunctionType.Copy
 
 P = 128
@@ -59,7 +61,8 @@ def tile_moe_sub_relu2_kernel(
         ident = keep.tile([P, P], F32, name="ident")
         y_sb = [keep.tile([P, SLOTS], F32, name="y_sb%d" % c, align_bytes=64) for c in range(PLANES)]
         gate_cols = keep.tile([P, 2 * BLOCKS], F32, name="gate_cols")
-        gate_sb = [keep.tile([P, T], F32, name="gate_sb%d" % r) for r in range(2)]
+        lead = keep.tile([P, BLOCKS], F32, name="lead")
+        ratio_sb = keep.tile([P, T], F32, name="ratio_sb")
         dh_rows = [keep.tile([P, PACK, P], F32, name="dh_rows%d" % b, align_bytes=64) for b in range(BLOCKS)]
         w1_codes = keep.tile([P, K], U32, name="w1_codes", align_bytes=64)
         w1_scales = keep.tile([P, K], U8, name="w1_scales", align_bytes=64)
@@ -133,14 +136,12 @@ def tile_moe_sub_relu2_kernel(
                 stop=(s == PASSES - 1),
             )
 
-        def weight_pass(e, s, c0, planes, accs, on_vector, lodging=None, raw=None):
+        def weight_pass(e, s, c0, planes, accs, on_vector, raw=None):
             if raw is None:
                 raw = load_rows(w2t[e, s * K_PASS : (s + 1) * K_PASS, :], c0, planes)
-            grouped, codes, scales = mx_tiles(planes * P, lodging)
+            grouped, codes, scales = mx_tiles(planes * P, None)
             round_rows(nc.vector.tensor_copy if on_vector else nc.scalar.copy, raw, grouped[:])
             nc.vector.quantize_mx(out=codes[:].bitcast(FP8X4), scales=scales[:], in_=grouped[:])
-            if e * C // GATHER not in gathered:
-                gather_dy(e * C // GATHER)
             for c in range(planes):
                 cols = slice(c * P, (c + 1) * P)
                 multiply(e, s, accs[c], codes[:, cols], scales[:, cols])
@@ -171,10 +172,8 @@ def tile_moe_sub_relu2_kernel(
                     if (e, s) == (E - 1, PASSES - 1):
                         last_pass(c0, accs, e0, "part11" if c0 == HALF else None)
                         return
-                    g = e * C // GATHER
-                    lodging = "slots%d" % (g + 1) if c0 == 0 and e % 2 == 1 and s == 0 and e < E - 1 else None
                     on_vector = c0 == 0 and (PASSES * e + s) % 2 == 0
-                    weight_pass(e, s, c0, planes, sums, on_vector, lodging, preloaded.get((e, s)))
+                    weight_pass(e, s, c0, planes, sums, on_vector, preloaded.get((e, s)))
             keep_sums(accs, c0, e0, e1)
 
         def spread_gates():
@@ -185,15 +184,33 @@ def tile_moe_sub_relu2_kernel(
             )
             turned = bank(4, [P, P])
             nc.tensor.transpose(turned[:], gate_rows[:], ident[:])
-            nc.scalar.activation(out=gate_cols[:], in_=turned[:, 0 : 2 * BLOCKS], func=COPY, scale=2.0)
-            for r in range(2):
-                for b0, nb in ((0, 4), (4, 1)):
-                    spread = bank(5 + r + b0 // 4, [P, nb * P])
-                    for b in range(nb):
-                        q = r * BLOCKS + b0 + b
-                        column = gate_cols[:, q : q + 1].to_broadcast([P, P])
-                        nc.tensor.transpose(spread[:, b * P : (b + 1) * P], column, ident[:])
-                    nc.scalar.copy(out=gate_sb[r][:, b0 * P : (b0 + nb) * P], in_=spread[:])
+            nc.scalar.copy(out=gate_cols[:], in_=turned[:, 0 : 2 * BLOCKS])
+            first, second = gate_cols[:, 0:BLOCKS], gate_cols[:, BLOCKS:]
+            size = keep.tile([P, 2 * BLOCKS], F32, name="size")
+            floor = keep.tile([P, BLOCKS], F32, name="floor")
+            small = keep.tile([P, BLOCKS], F32, name="small")
+            lift = keep.tile([P, BLOCKS], F32, name="lift")
+            safe = keep.tile([P, BLOCKS], F32, name="safe")
+            ratio = keep.tile([P, BLOCKS], F32, name="ratio")
+            nc.vector.scalar_tensor_tensor(
+                out=size[:], in0=gate_cols[:], scalar=-1.0, in1=gate_cols[:], op0=MULT, op1=MAX
+            )
+            nc.vector.tensor_scalar(
+                out=floor[:], in0=size[:, BLOCKS:], scalar1=2.0**-30, scalar2=2.0**-100, op0=MULT, op1=MAX
+            )
+            nc.vector.tensor_tensor(out=small[:], in0=size[:, 0:BLOCKS], in1=floor[:], op=IS_LT)
+            nc.vector.tensor_tensor(out=lift[:], in0=floor[:], in1=first, op=SUBTRACT)
+            nc.vector.tensor_tensor(out=lift[:], in0=lift[:], in1=small[:], op=MULT)
+            nc.vector.tensor_tensor(out=safe[:], in0=first, in1=lift[:], op=ADD)
+            nc.vector.reciprocal(out=ratio[:], in_=safe[:])
+            nc.vector.tensor_tensor(out=ratio[:], in0=ratio[:], in1=second, op=MULT)
+            nc.scalar.activation(out=lead[:], in_=safe[:], func=COPY, scale=2.0)
+            for b0, nb in ((0, 4), (4, 1)):
+                spread = bank(5 + b0 // 4, [P, nb * P])
+                for b in range(nb):
+                    column = ratio[:, b0 + b : b0 + b + 1].to_broadcast([P, P])
+                    nc.tensor.transpose(spread[:, b * P : (b + 1) * P], column, ident[:])
+                nc.scalar.copy(out=ratio_sb[:, b0 * P : (b0 + nb) * P], in_=spread[:])
 
         parts = {}
 
@@ -208,9 +225,12 @@ def tile_moe_sub_relu2_kernel(
         def fetch_weighted(c0, planes, r, b0, nb):
             part = keep.tile([P, planes, nb * P], F32, name="part", tag="part%d%d" % (c0 + b0, r), align_bytes=64)
             for c in range(planes):
-                nc.vector.tensor_tensor(
-                    out=part[:, c, :], in0=window(c0 + c, r, b0, nb), in1=gate_sb[r][:, b0 * P : (b0 + nb) * P], op=MULT
-                )
+                if r == 0:
+                    nc.vector.tensor_copy(out=part[:, c, :], in_=window(c0 + c, r, b0, nb))
+                else:
+                    nc.vector.tensor_tensor(
+                        out=part[:, c, :], in0=window(c0 + c, r, b0, nb), in1=ratio_sb[:, b0 * P : (b0 + nb) * P], op=MULT
+                    )
             note_parts(part[:], c0, r, b0, nb)
 
         def fetch_plain(r, b0, nb):
@@ -218,11 +238,6 @@ def tile_moe_sub_relu2_kernel(
             for c in range(HALF):
                 nc.scalar.activation(out=part[:, c, :], in_=window(HALF + c, r, b0, nb), func=COPY)
             note_parts(part[:], HALF, r, b0, nb)
-            return part
-
-        def weigh(part, r, b0, nb):
-            weight = gate_sb[r][:, b0 * P : (b0 + nb) * P].unsqueeze(1).to_broadcast([P, HALF, nb * P])
-            nc.vector.tensor_tensor(out=part[:], in0=part[:], in1=weight, op=MULT)
 
         turned = {}
 
@@ -242,7 +257,9 @@ def tile_moe_sub_relu2_kernel(
 
         def finish_rows(b):
             turn(range(HALF, PLANES), 0, [b])
-            nc.scalar.copy(out=dh_rows[b][:], in_=turned[b][:].rearrange("p (m t) -> p t m", t=PACK))
+            nc.scalar.activation(
+                out=dh_rows[b][:], in_=turned[b][:].rearrange("p (m t) -> p t m", t=PACK), func=COPY, scale=lead[:, b : b + 1]
+            )
 
         da_grouped = [
             keep.tile([P, n, PACK], BF16, name="da_grouped", tag="bf16_piece%d" % n0, align_bytes=64) for n0, n in PIECES
@@ -341,6 +358,8 @@ def tile_moe_sub_relu2_kernel(
         for q in range(4):
             load_scales(q)
         make_identity(nc, ident[:])
+        for g in range(SLOTS // GATHER):
+            gather_dy(g)
 
         expert_group(*GROUPS[0], 0, PLANES, 0, first)
         nc.sync.dma_start(pos_sb[0][:], pos1)
@@ -359,18 +378,15 @@ def tile_moe_sub_relu2_kernel(
             for r in range(2):
                 fetch_weighted(c, 1, r, 0, BLOCKS)
                 turn([c], r, range(BLOCKS))
-        plain = fetch_plain(0, *CHUNKS[0])
+        fetch_plain(0, *CHUNKS[0])
         fetch_weighted(HALF, HALF, 1, *CHUNKS[0])
         turn(range(HALF, PLANES), 1, (0, 1))
-        weigh(plain, 0, *CHUNKS[0])
-        plain = fetch_plain(0, *CHUNKS[1])
-        last_plain = fetch_plain(0, *CHUNKS[2])
+        fetch_plain(0, *CHUNKS[1])
+        fetch_plain(0, *CHUNKS[2])
         finish_rows(0)
         finish_rows(1)
         fetch_weighted(HALF, HALF, 1, *CHUNKS[1])
-        weigh(plain, 0, *CHUNKS[1])
         fetch_weighted(HALF, HALF, 1, *CHUNKS[2])
-        weigh(last_plain, 0, *CHUNKS[2])
         make_da(0, a_sb)
         turn(range(HALF, PLANES), 1, (2, 3, 4))
         w1_grouped = keep.tile([P, K * PACK], BF16, name="w1_grouped", tag="part20", align_bytes=64)

@@ -213,6 +213,7 @@ def tile_moe_sub_relu2_kernel(
                 nc.scalar.copy(out=ratio_sb[:, b0 * P : (b0 + nb) * P], in_=spread[:])
 
         parts = {}
+        seconds = {}
 
         def window(c, r, b0, nb):
             return y_sb[c][:].indirect(pos_sb[r][:, b0 * P // LIST_COL : (b0 + nb) * P // LIST_COL])
@@ -231,13 +232,18 @@ def tile_moe_sub_relu2_kernel(
                     nc.vector.tensor_tensor(
                         out=part[:, c, :], in0=window(c0 + c, r, b0, nb), in1=ratio_sb[:, b0 * P : (b0 + nb) * P], op=MULT
                     )
+                seconds[c0 + c, b0] = part[:, c, :]
             note_parts(part[:], c0, r, b0, nb)
 
-        def fetch_plain(r, b0, nb):
-            part = keep.tile([P, HALF, nb * P], F32, name="part", tag="part%d%d" % (HALF + b0, r), align_bytes=64)
-            for c in range(HALF):
-                nc.scalar.activation(out=part[:, c, :], in_=window(HALF + c, r, b0, nb), func=COPY)
-            note_parts(part[:], HALF, r, b0, nb)
+        def fetch_plain(c, b0, nb):
+            part = keep.tile([P, 1, nb * P], F32, name="part", tag="first%d%d" % (c, b0), align_bytes=64)
+            nc.scalar.activation(out=part[:, 0, :], in_=window(c, 0, b0, nb), func=COPY)
+            note_parts(part[:], c, 0, b0, nb)
+
+        def fetch_onto(c, b0, nb):
+            part = keep.tile([P, 1, nb * P], F32, name="part", tag="first%d%d" % (c, b0), align_bytes=64)
+            nc.vector.tensor_tensor(out=part[:, 0, :], in0=window(c, 0, b0, nb), in1=seconds[c, b0], op=ADD)
+            note_parts(part[:], c, 0, b0, nb)
 
         turned = {}
 
@@ -378,18 +384,21 @@ def tile_moe_sub_relu2_kernel(
             for r in range(2):
                 fetch_weighted(c, 1, r, 0, BLOCKS)
                 turn([c], r, range(BLOCKS))
-        fetch_plain(0, *CHUNKS[0])
+        fetch_plain(2, *CHUNKS[0])
+        fetch_plain(3, *CHUNKS[0])
         fetch_weighted(HALF, HALF, 1, *CHUNKS[0])
         turn(range(HALF, PLANES), 1, (0, 1))
-        fetch_plain(0, *CHUNKS[1])
-        fetch_plain(0, *CHUNKS[2])
+        fetch_plain(2, *CHUNKS[1])
+        fetch_plain(3, *CHUNKS[1])
         finish_rows(0)
         finish_rows(1)
         fetch_weighted(HALF, HALF, 1, *CHUNKS[1])
         fetch_weighted(HALF, HALF, 1, *CHUNKS[2])
+        fetch_onto(2, *CHUNKS[2])
+        fetch_onto(3, *CHUNKS[2])
         make_da(0, a_sb)
-        turn(range(HALF, PLANES), 1, (2, 3, 4))
-        w1_grouped = keep.tile([P, K * PACK], BF16, name="w1_grouped", tag="part20", align_bytes=64)
+        turn(range(HALF, PLANES), 1, (2, 3))
+        w1_grouped = keep.tile([P, K * PACK], BF16, name="w1_grouped", tag="first30", align_bytes=64)
         for copy, words in ((nc.scalar.copy, slice(0, P // 2)), (nc.vector.tensor_copy, slice(P // 2, P))):
             copy(
                 out=w1_grouped[:].rearrange("p (t m j) -> p m j t", t=PACK, j=PACK)[:, words],

@@ -33,6 +33,7 @@ CHUNKS = ((0, 2), (2, 2), (4, 1))
 BLOCKS = T // P
 GROUPS = ((0, 3), (3, 7), (7, 8))
 BANK = 512
+WARM_PASSES = 4
 WHOLE_LOADS = 6
 EXPERT_SLOTS = 3
 EXPERT_BYTES = PASSES * PACK * H * 4
@@ -113,6 +114,7 @@ def tile_moe_sub_relu2_kernel(
             copy(out=grouped.rearrange("p (c i j) -> p c j i", i=4, j=PACK), in_=raw.rearrange("p j (c i) -> p c j i", i=4))
 
         gathered = {}
+        last_codes = {}
 
         def gather_dy(g):
             offsets = offs_sb[:, g * GATHER // LIST_COL : (g + 1) * GATHER // LIST_COL]
@@ -149,6 +151,7 @@ def tile_moe_sub_relu2_kernel(
         def last_pass(c0, accs, e0, lodging):
             raw = load_rows(w2t[E - 1, (PASSES - 1) * K_PASS :, :], c0, HALF)
             grouped, codes, scales = mx_tiles(HALF * P, lodging)
+            last_codes[c0] = (codes, scales)
             for c in range(HALF):
                 cols = slice(c * P, (c + 1) * P)
                 words = slice(c * K_PASS, (c + 1) * K_PASS)
@@ -307,6 +310,20 @@ def tile_moe_sub_relu2_kernel(
                     op1=MULT,
                 )
 
+        def warm_up():
+            codes, scales = last_codes[HALF]
+            unread = bank(BACK_BANKS[0], [P, HALF * P])
+            for repeat in range(WARM_PASSES):
+                nc.tensor.matmul_mx(
+                    out=unread[:],
+                    lhsT=codes[:, 0:P].bitcast(FP8X4),
+                    lhsT_scale=scales[:, 0:P],
+                    rhs=codes[:].bitcast(FP8X4),
+                    rhs_scale=scales[:],
+                    start=True,
+                    stop=True,
+                )
+
         def quantize_da(k):
             nc.vector.quantize_mx(
                 out=da_codes[:, columns(k)].bitcast(FP8X4),
@@ -397,6 +414,7 @@ def tile_moe_sub_relu2_kernel(
         fetch_onto(2, *CHUNKS[2])
         fetch_onto(3, *CHUNKS[2])
         make_da(0, a_sb)
+        warm_up()
         turn(range(HALF, PLANES), 1, (2, 3))
         w1_grouped = keep.tile([P, K * PACK], BF16, name="w1_grouped", tag="first30", align_bytes=64)
         for copy, words in ((nc.scalar.copy, slice(0, P // 2)), (nc.vector.tensor_copy, slice(P // 2, P))):

@@ -33,7 +33,7 @@ CHUNKS = ((0, 2), (2, 2), (4, 1))
 BLOCKS = T // P
 GROUPS = ((0, 3), (3, 7), (7, 8))
 BANK = 512
-WARM_PASSES = 4
+WARM_PASSES = 7
 WHOLE_LOADS = 6
 EXPERT_SLOTS = 3
 EXPERT_BYTES = PASSES * PACK * H * 4

@@ -57,8 +57,8 @@ def tile_moe_sub_relu2_kernel(
 
         offs_sb = keep.tile([P, SLOTS // LIST_COL], U16, name="offs_sb")
         pos_sb = [keep.tile([P, T // LIST_COL], U16, name="pos_sb%d" % r) for r in range(2)]
-        dy_word_sb = keep.tile([P, PASSES, T], I32, name="dy_word_sb", align_bytes=64)
-        dy_scale_sb = keep.tile([P, T], U8, name="dy_scale_sb", align_bytes=64)
+        dy_word_sb = keep.tile([P, PASSES, T], I32, name="dy_word_sb", align_bytes=256)
+        dy_scale_sb = keep.tile([P, T], U8, name="dy_scale_sb", align_bytes=256)
         ident = keep.tile([P, P], F32, name="ident")
         y_sb = [keep.tile([P, SLOTS], F32, name="y_sb%d" % c, align_bytes=64) for c in range(PLANES)]
         gate_cols = keep.tile([P, 2 * BLOCKS], F32, name="gate_cols")
@@ -67,8 +67,8 @@ def tile_moe_sub_relu2_kernel(
         dh_rows = [keep.tile([P, PACK, P], F32, name="dh_rows%d" % b, align_bytes=64) for b in range(BLOCKS)]
         w1_codes = keep.tile([P, K], U32, name="w1_codes", align_bytes=64)
         w1_scales = keep.tile([P, K], U8, name="w1_scales", align_bytes=64)
-        out_codes = keep.tile([P, T], I32, name="out_codes", align_bytes=64)
-        out_scales = keep.tile([P, T], U8, name="out_scales", align_bytes=64)
+        out_codes = keep.tile([P, T], I32, name="out_codes", align_bytes=256)
+        out_scales = keep.tile([P, T], U8, name="out_scales", align_bytes=256)
 
         def bank(i, shape):
             return psum.tile(shape, F32, name="bank", tag="bank%d" % i)
@@ -78,12 +78,12 @@ def tile_moe_sub_relu2_kernel(
         def stage_tile(shape):
             slot = len(staged) % STAGE_SLOTS
             staged.append(slot)
-            return stage.tile(shape, F32, name="raw", tag="raw%d" % slot, offset=slot * SLOT_BYTES, align_bytes=64)
+            return stage.tile(shape, F32, name="raw", tag="raw%d" % slot, offset=slot * SLOT_BYTES, align_bytes=256)
 
         def load_expert(e):
             slot = e % EXPERT_SLOTS
             raw = stage.tile(
-                [P, PASSES, PACK, H], F32, name="expert", tag="expert%d" % slot, offset=slot * EXPERT_BYTES, align_bytes=64
+                [P, PASSES, PACK, H], F32, name="expert", tag="expert%d" % slot, offset=slot * EXPERT_BYTES, align_bytes=256
             )
             nc.sync.dma_start(
                 out=raw[:].rearrange("p s j h -> p s (j h)"), in_=w2t[e].rearrange("(s p j) h -> p s (j h)", p=P, j=PACK)
@@ -275,7 +275,7 @@ def tile_moe_sub_relu2_kernel(
         ]
         da_codes = keep.tile([P, T], U32, name="da_codes", align_bytes=64)
         da_scales = keep.tile([P, T], U8, name="da_scales", align_bytes=64)
-        results = [keep.tile([P, PACK, nb * P], F32, name="result%d" % b0, align_bytes=64) for b0, nb in CHUNKS]
+        results = [keep.tile([P, PACK, nb * P], F32, name="result%d" % b0, align_bytes=256) for b0, nb in CHUNKS]
         rounded = [
             keep.tile([P, nb * P, PACK], BF16, name="rounded", tag="bf16_piece%d" % (b0 * P), align_bytes=64)
             for b0, nb in CHUNKS
@@ -393,6 +393,7 @@ def tile_moe_sub_relu2_kernel(
         expert_group(E - 2, E - 1, 0, HALF, 4, {})
         expert_group(E - 1, E, 0, HALF, 6, {})
         expert_group(E - 2, E, HALF, HALF, 0, {})
+        warm_up()
         w1_raw = load_rows(w1t, 0, PLANES)
         a_sb = stage_tile([P, PACK, T])
         nc.sync.dma_start(out=a_sb[:].rearrange("p t n -> p (t n)"), in_=a.rearrange("(p t) n -> p (t n)", t=PACK))
@@ -414,7 +415,6 @@ def tile_moe_sub_relu2_kernel(
         fetch_onto(2, *CHUNKS[2])
         fetch_onto(3, *CHUNKS[2])
         make_da(0, a_sb)
-        warm_up()
         turn(range(HALF, PLANES), 1, (2, 3))
         w1_grouped = keep.tile([P, K * PACK], BF16, name="w1_grouped", tag="first30", align_bytes=64)
         for copy, words in ((nc.scalar.copy, slice(0, P // 2)), (nc.vector.tensor_copy, slice(P // 2, P))):

@@ -34,9 +34,6 @@ BLOCKS = T // P
 GROUPS = ((0, 3), (3, 7), (7, 8))
 BANK = 512
 WARM_PASSES = 7
-WHOLE_LOADS = 6
-EXPERT_SLOTS = 3
-EXPERT_BYTES = PASSES * PACK * H * 4
 STAGE_SLOTS = 8
 SLOT_BYTES = PACK * T * 4
 TOKEN_BANK0 = 2
@@ -79,16 +76,6 @@ def tile_moe_sub_relu2_kernel(
             slot = len(staged) % STAGE_SLOTS
             staged.append(slot)
             return stage.tile(shape, F32, name="raw", tag="raw%d" % slot, offset=slot * SLOT_BYTES, align_bytes=256)
-
-        def load_expert(e):
-            slot = e % EXPERT_SLOTS
-            raw = stage.tile(
-                [P, PASSES, PACK, H], F32, name="expert", tag="expert%d" % slot, offset=slot * EXPERT_BYTES, align_bytes=256
-            )
-            nc.sync.dma_start(
-                out=raw[:].rearrange("p s j h -> p s (j h)"), in_=w2t[e].rearrange("(s p j) h -> p s (j h)", p=P, j=PACK)
-            )
-            return {(e, s): raw[:, s] for s in range(PASSES)}
 
         def load_rows(rows, c0, planes):
             raw = stage_tile([P, PACK, planes * P])
@@ -168,14 +155,12 @@ def tile_moe_sub_relu2_kernel(
         def expert_group(e0, e1, c0, planes, bank0, preloaded):
             accs = [bank(bank0 + c, [P, BANK]) for c in range(planes)]
             for e in range(e0, e1):
-                if 0 < e < WHOLE_LOADS:
-                    preloaded = load_expert(e)
                 sums = [acc[:, (e - e0) * C : (e - e0 + 1) * C] for acc in accs]
                 for s in range(PASSES):
                     if (e, s) == (E - 1, PASSES - 1):
                         last_pass(c0, accs, e0, "part11" if c0 == HALF else None)
                         return
-                    on_vector = c0 == 0 and (PASSES * e + s) % 2 == 0
+                    on_vector = c0 == 0 and (PASSES * e + s) % 2 == 0 and (e, s) != (0, PASSES - 1)
                     weight_pass(e, s, c0, planes, sums, on_vector, preloaded.get((e, s)))
             keep_sums(accs, c0, e0, e1)
 
@@ -368,6 +353,11 @@ def tile_moe_sub_relu2_kernel(
                 in_=rounded[chunk][:].rearrange("p n t -> p (n t)"),
             )
 
+        def store_scales(queue, q, cols):
+            queue.dma_start(
+                out=out_2[0, 4 * q : 4 * q + 4, cols].bitcast(I32), in_=out_scales[32 * q : 32 * q + 4, cols].bitcast(I32)
+            )
+
         def load_scales(q):
             nc.sync.dma_start(
                 out=dy_scale_sb[32 * q : 32 * q + 4 * PASSES, :].bitcast(I32),
@@ -375,7 +365,7 @@ def tile_moe_sub_relu2_kernel(
             )
 
         nc.vector.memset(dy_scale_sb[:].bitcast(I32), 0)
-        first = load_expert(0)
+        first = {(0, 0): load_rows(w2t[0, 0:K_PASS, :], 0, PLANES)}
         nc.sync.dma_start(out=dy_word_sb[:], in_=dy_words.rearrange("s p n d -> p s (n d)").bitcast(I32))
         nc.sync.dma_start(offs_sb[:], offs)
         for q in range(4):
@@ -434,20 +424,19 @@ def tile_moe_sub_relu2_kernel(
         for k in (2, 3):
             make_da(k, a_sb)
             quantize_da(k)
+        words_out = out_1[0].rearrange("p n d -> p (n d)").bitcast(I32)
+        head = CHUNKS[0][1] * P
+        quantize_result(0)
+        nc.sync.dma_start(out=words_out[:, 0:head], in_=out_codes[:, 0:head])
+        store_scales(nc.sync, 0, slice(0, head))
         project(1)
         store(1, slice(0, 2))
         store(1, slice(2, PACK))
         project(2)
         project(3)
         store(2, slice(0, PACK))
-        words_out = out_1[0].rearrange("p n d -> p (n d)").bitcast(I32)
-        quantize_result(0)
         quantize_result(1)
-        nc.scalar.dma_start(out=words_out[:, 0 : 4 * P], in_=out_codes[:, 0 : 4 * P])
         quantize_result(2)
-        nc.scalar.dma_start(out=words_out[:, 4 * P :], in_=out_codes[:, 4 * P :])
+        nc.sync.dma_start(out=words_out[:, head:], in_=out_codes[:, head:])
         for q in range(4):
-            queue = nc.sync if q % 2 == 0 else nc.scalar
-            queue.dma_start(
-                out=out_2[0, 4 * q : 4 * q + 4, :].bitcast(I32), in_=out_scales[32 * q : 32 * q + 4, :].bitcast(I32)
-            )
+            store_scales(nc.sync, q, slice(head if q == 0 else 0, T))

@@ -33,7 +33,6 @@ CHUNKS = ((0, 2), (2, 2), (4, 1))
 BLOCKS = T // P
 GROUPS = ((0, 3), (3, 7), (7, 8))
 BANK = 512
-WARM_PASSES = 7
 STAGE_SLOTS = 8
 SLOT_BYTES = PACK * T * 4
 TOKEN_BANK0 = 2
@@ -101,7 +100,6 @@ def tile_moe_sub_relu2_kernel(
             copy(out=grouped.rearrange("p (c i j) -> p c j i", i=4, j=PACK), in_=raw.rearrange("p j (c i) -> p c j i", i=4))
 
         gathered = {}
-        last_codes = {}
 
         def gather_dy(g):
             offsets = offs_sb[:, g * GATHER // LIST_COL : (g + 1) * GATHER // LIST_COL]
@@ -138,7 +136,6 @@ def tile_moe_sub_relu2_kernel(
         def last_pass(c0, accs, e0, lodging):
             raw = load_rows(w2t[E - 1, (PASSES - 1) * K_PASS :, :], c0, HALF)
             grouped, codes, scales = mx_tiles(HALF * P, lodging)
-            last_codes[c0] = (codes, scales)
             for c in range(HALF):
                 cols = slice(c * P, (c + 1) * P)
                 words = slice(c * K_PASS, (c + 1) * K_PASS)
@@ -295,20 +292,6 @@ def tile_moe_sub_relu2_kernel(
                     op1=MULT,
                 )
 
-        def warm_up():
-            codes, scales = last_codes[HALF]
-            unread = bank(BACK_BANKS[0], [P, HALF * P])
-            for repeat in range(WARM_PASSES):
-                nc.tensor.matmul_mx(
-                    out=unread[:],
-                    lhsT=codes[:, 0:P].bitcast(FP8X4),
-                    lhsT_scale=scales[:, 0:P],
-                    rhs=codes[:].bitcast(FP8X4),
-                    rhs_scale=scales[:],
-                    start=True,
-                    stop=True,
-                )
-
         def quantize_da(k):
             nc.vector.quantize_mx(
                 out=da_codes[:, columns(k)].bitcast(FP8X4),
@@ -383,7 +366,6 @@ def tile_moe_sub_relu2_kernel(
         expert_group(E - 2, E - 1, 0, HALF, 4, {})
         expert_group(E - 1, E, 0, HALF, 6, {})
         expert_group(E - 2, E, HALF, HALF, 0, {})
-        warm_up()
         w1_raw = load_rows(w1t, 0, PLANES)
         a_sb = stage_tile([P, PACK, T])
         nc.sync.dma_start(out=a_sb[:].rearrange("p t n -> p (t n)"), in_=a.rearrange("(p t) n -> p (t n)", t=PACK))

from contextlib import ExitStack

import concourse.mybir as mybir
from concourse.masks import make_identity

K, T, E, C, H, N = 512, 640, 10, 128, 512, 1536
FLOPS = 2 * E * C * N * H + 2 * T * H * K

F32 = mybir.dt.float32
BF16 = mybir.dt.bfloat16
I32 = mybir.dt.int32
U32 = mybir.dt.uint32
U16 = mybir.dt.uint16
U8 = mybir.dt.uint8
FP8X4 = mybir.dt.float8_e4m3fn_x4
MULT = mybir.AluOpType.mult
ADD = mybir.AluOpType.add
MAX = mybir.AluOpType.max
SUBTRACT = mybir.AluOpType.subtract
IS_LT = mybir.AluOpType.is_lt
COPY = mybir.ActivationFunctionType.Copy

P = 128
PACK = 4
K_PASS = P * PACK
PASSES = N // K_PASS
PLANES = H // P
HALF = PLANES // 2
SLOTS = E * C
LIST_COL = 16
GATHER = 2 * C
CHUNKS = ((0, 2), (2, 2), (4, 1))
BLOCKS = T // P
GROUPS = ((0, 3), (3, 7), (7, 8))
BANK = 512
STAGE_SLOTS = 8
SLOT_BYTES = PACK * T * 4
TOKEN_BANK0 = 2
BACK_BANKS = (7, 0, 1, 7, 0)
PIECES = ((0, 256), (256, 256), (512, 64), (576, 64))
OUT_BANKS = ((2, 3), (4, 5), (6,), (7,))


def tile_moe_sub_relu2_kernel(
    tc, dy_words, dy_scales, w2t, w1t, a, gate, offs, pos1, pos2, out_0, out_1, out_2
):
    nc = tc.nc
    with ExitStack() as ctx:
        keep = ctx.enter_context(tc.tile_pool(name="keep", bufs=1))
        ring = ctx.enter_context(tc.tile_pool(name="ring", bufs=1))
        stage = ctx.enter_context(tc.tile_pool(name="stage", bufs=1))
        psum = ctx.enter_context(tc.psum_pool(name="psum", bufs=1))

        offs_sb = keep.tile([P, SLOTS // LIST_COL], U16, name="offs_sb")
        pos_sb = [keep.tile([P, T // LIST_COL], U16, name="pos_sb%d" % r) for r in range(2)]
        dy_word_sb = keep.tile([P, PASSES, T], I32, name="dy_word_sb", align_bytes=256)
        dy_scale_sb = keep.tile([P, T], U8, name="dy_scale_sb", align_bytes=256)
        ident = keep.tile([P, P], F32, name="ident")
        y_sb = [keep.tile([P, SLOTS], F32, name="y_sb%d" % c, align_bytes=64) for c in range(PLANES)]
        gate_cols = keep.tile([P, 2 * BLOCKS], F32, name="gate_cols")
        lead = keep.tile([P, BLOCKS], F32, name="lead")
        ratio_sb = keep.tile([P, T], F32, name="ratio_sb")
        dh_rows = [keep.tile([P, PACK, P], F32, name="dh_rows%d" % b, align_bytes=64) for b in range(BLOCKS)]
        w1_codes = keep.tile([P, K], U32, name="w1_codes", align_bytes=64)
        w1_scales = keep.tile([P, K], U8, name="w1_scales", align_bytes=64)
        out_codes = keep.tile([P, T], I32, name="out_codes", align_bytes=256)
        out_scales = keep.tile([P, T], U8, name="out_scales", align_bytes=256)

        def bank(i, shape):
            return psum.tile(shape, F32, name="bank", tag="bank%d" % i)

        staged = []

        def stage_tile(shape):
            slot = len(staged) % STAGE_SLOTS
            staged.append(slot)
            return stage.tile(shape, F32, name="raw", tag="raw%d" % slot, offset=slot * SLOT_BYTES, align_bytes=256)

        def load_rows(rows, c0, planes):
            raw = stage_tile([P, PACK, planes * P])
            if planes == PLANES:
                nc.sync.dma_start(
                    out=raw[:].rearrange("p j h -> p (j h)"), in_=rows.rearrange("(p j) h -> p (j h)", j=PACK)
                )
            else:
                rows = rows.rearrange("(p j) h -> p j h", j=PACK)
                nc.sync.dma_start(out=raw[:], in_=rows[:, :, c0 * P : (c0 + planes) * P])
            return raw[:]

        def mx_tiles(words, lodging):
            if lodging is None:
                grouped = ring.tile([P, words * PACK], BF16, name="grouped", bufs=6, align_bytes=64)
            else:
                grouped = keep.tile([P, words * PACK], BF16, name="early", tag=lodging, align_bytes=64)
            codes = ring.tile([P, words], U32, name="codes", bufs=7, align_bytes=64)
            scales = ring.tile([P, words], U8, name="scales", bufs=7, align_bytes=64)
            return grouped, codes, scales

        def round_rows(copy, raw, grouped):
            copy(out=grouped.rearrange("p (c i j) -> p c j i", i=4, j=PACK), in_=raw.rearrange("p j (c i) -> p c j i", i=4))

        gathered = {}

        def gather_dy(g):
            offsets = offs_sb[:, g * GATHER // LIST_COL : (g + 1) * GATHER // LIST_COL]
            words = keep.tile([P, PASSES, GATHER], U32, name="slot_words", tag="slots%d" % g, align_bytes=64)
            for s in range(PASSES):
                nc.vector.tensor_copy(out=words[:, s, :], in_=dy_word_sb[:, s, :].bitcast(U32).indirect(offsets))
            z = keep.tile([P, GATHER], U8, name="slot_scales%d" % g, align_bytes=64)
            nc.vector.tensor_copy(out=z[:], in_=dy_scale_sb[:].indirect(offsets))
            gathered[g] = (words, z)

        def multiply(e, s, acc, codes, scales):
            words, z = gathered[e * C // GATHER]
            cols = slice(e * C % GATHER, e * C % GATHER + C)
            nc.tensor.matmul_mx(
                out=acc,
                lhsT=codes.bitcast(FP8X4),
                lhsT_scale=scales,
                rhs=words[:, s, cols].bitcast(FP8X4),
                rhs_scale=z[4 * s : P, cols],
                start=(s == 0),
                stop=(s == PASSES - 1),
            )

        def weight_pass(e, s, c0, planes, accs, on_vector, raw=None):
            if raw is None:
                raw = load_rows(w2t[e, s * K_PASS : (s + 1) * K_PASS, :], c0, planes)
            grouped, codes, scales = mx_tiles(planes * P, None)
            round_rows(nc.vector.tensor_copy if on_vector else nc.scalar.copy, raw, grouped[:])
            nc.vector.quantize_mx(out=codes[:].bitcast(FP8X4), scales=scales[:], in_=grouped[:])
            for c in range(planes):
                cols = slice(c * P, (c + 1) * P)
                multiply(e, s, accs[c], codes[:, cols], scales[:, cols])

        def last_pass(c0, accs, e0, lodging):
            raw = load_rows(w2t[E - 1, (PASSES - 1) * K_PASS :, :], c0, HALF)
            grouped, codes, scales = mx_tiles(HALF * P, lodging)
            for c in range(HALF):
                cols = slice(c * P, (c + 1) * P)
                words = slice(c * K_PASS, (c + 1) * K_PASS)
                round_rows(nc.vector.tensor_copy if c == 0 else nc.scalar.copy, raw[:, :, cols], grouped[:, words])
                nc.vector.quantize_mx(out=codes[:, cols].bitcast(FP8X4), scales=scales[:, cols], in_=grouped[:, words])
                multiply(E - 1, PASSES - 1, accs[c][:, (E - 1 - e0) * C : (E - e0) * C], codes[:, cols], scales[:, cols])
                copy = nc.vector.tensor_copy if c0 + c == 0 else nc.scalar.copy
                copy(out=y_sb[c0 + c][:, e0 * C :], in_=accs[c][:, 0 : (E - e0) * C])

        def keep_sums(accs, c0, e0, e1):
            for c, acc in enumerate(accs):
                nc.scalar.copy(out=y_sb[c0 + c][:, e0 * C : e1 * C], in_=acc[:, 0 : (e1 - e0) * C])

        def expert_group(e0, e1, c0, planes, bank0, preloaded):
            accs = [bank(bank0 + c, [P, BANK]) for c in range(planes)]
            for e in range(e0, e1):
                sums = [acc[:, (e - e0) * C : (e - e0 + 1) * C] for acc in accs]
                for s in range(PASSES):
                    if (e, s) == (E - 1, PASSES - 1):
                        last_pass(c0, accs, e0, "part11" if c0 == HALF else None)
                        return
                    on_vector = c0 == 0 and (PASSES * e + s) % 2 == 0 and (e, s) != (0, PASSES - 1)
                    weight_pass(e, s, c0, planes, sums, on_vector, preloaded.get((e, s)))
            keep_sums(accs, c0, e0, e1)

        def spread_gates():
            gate_rows = keep.tile([P, P], F32, name="gate_rows")
            nc.gpsimd.memset(gate_rows[:], 0.0)
            nc.sync.dma_start(
                out=gate_rows[0 : 2 * BLOCKS, :], in_=gate[:, 0, :].rearrange("r (b n) -> r b n", n=P)
            )
            turned = bank(4, [P, P])
            nc.tensor.transpose(turned[:], gate_rows[:], ident[:])
            nc.scalar.copy(out=gate_cols[:], in_=turned[:, 0 : 2 * BLOCKS])
            first, second = gate_cols[:, 0:BLOCKS], gate_cols[:, BLOCKS:]
            size = keep.tile([P, 2 * BLOCKS], F32, name="size")
            floor = keep.tile([P, BLOCKS], F32, name="floor")
            small = keep.tile([P, BLOCKS], F32, name="small")
            lift = keep.tile([P, BLOCKS], F32, name="lift")
            safe = keep.tile([P, BLOCKS], F32, name="safe")
            ratio = keep.tile([P, BLOCKS], F32, name="ratio")
            nc.vector.scalar_tensor_tensor(
                out=size[:], in0=gate_cols[:], scalar=-1.0, in1=gate_cols[:], op0=MULT, op1=MAX
            )
            nc.vector.tensor_scalar(
                out=floor[:], in0=size[:, BLOCKS:], scalar1=2.0**-30, scalar2=2.0**-100, op0=MULT, op1=MAX
            )
            nc.vector.tensor_tensor(out=small[:], in0=size[:, 0:BLOCKS], in1=floor[:], op=IS_LT)
            nc.vector.tensor_tensor(out=lift[:], in0=floor[:], in1=first, op=SUBTRACT)
            nc.vector.tensor_tensor(out=lift[:], in0=lift[:], in1=small[:], op=MULT)
            nc.vector.tensor_tensor(out=safe[:], in0=first, in1=lift[:], op=ADD)
            nc.vector.reciprocal(out=ratio[:], in_=safe[:])
            nc.vector.tensor_tensor(out=ratio[:], in0=ratio[:], in1=second, op=MULT)
            nc.scalar.activation(out=lead[:], in_=safe[:], func=COPY, scale=2.0)
            for b0, nb in ((0, 4), (4, 1)):
                spread = bank(5 + b0 // 4, [P, nb * P])
                for b in range(nb):
                    column = ratio[:, b0 + b : b0 + b + 1].to_broadcast([P, P])
                    nc.tensor.transpose(spread[:, b * P : (b + 1) * P], column, ident[:])
                nc.scalar.copy(out=ratio_sb[:, b0 * P : (b0 + nb) * P], in_=spread[:])

        parts = {}
        seconds = {}

        def window(c, r, b0, nb):
            return y_sb[c][:].indirect(pos_sb[r][:, b0 * P // LIST_COL : (b0 + nb) * P // LIST_COL])

        def note_parts(part, c0, r, b0, nb):
            for c in range(part.shape[1]):
                for b in range(nb):
                    parts[c0 + c, r, b0 + b] = part[:, c, b * P : (b + 1) * P]

        def fetch_weighted(c0, planes, r, b0, nb):
            part = keep.tile([P, planes, nb * P], F32, name="part", tag="part%d%d" % (c0 + b0, r), align_bytes=64)
            for c in range(planes):
                if r == 0:
                    nc.vector.tensor_copy(out=part[:, c, :], in_=window(c0 + c, r, b0, nb))
                else:
                    nc.vector.tensor_tensor(
                        out=part[:, c, :], in0=window(c0 + c, r, b0, nb), in1=ratio_sb[:, b0 * P : (b0 + nb) * P], op=MULT
                    )
                seconds[c0 + c, b0] = part[:, c, :]
            note_parts(part[:], c0, r, b0, nb)

        def fetch_plain(c, b0, nb):
            part = keep.tile([P, 1, nb * P], F32, name="part", tag="first%d%d" % (c, b0), align_bytes=64)
            nc.scalar.activation(out=part[:, 0, :], in_=window(c, 0, b0, nb), func=COPY)
            note_parts(part[:], c, 0, b0, nb)

        def fetch_onto(c, b0, nb):
            part = keep.tile([P, 1, nb * P], F32, name="part", tag="first%d%d" % (c, b0), align_bytes=64)
            nc.vector.tensor_tensor(out=part[:, 0, :], in0=window(c, 0, b0, nb), in1=seconds[c, b0], op=ADD)
            note_parts(part[:], c, 0, b0, nb)

        turned = {}

        def turn(planes, r, blocks):
            for b in blocks:
                if b not in turned:
                    turned[b] = bank(TOKEN_BANK0 + b, [P, H])
                for c in planes:
                    nc.tensor.matmul(
                        turned[b][:, c * P : (c + 1) * P],
                        lhsT=parts[c, r, b],
                        rhs=ident[:],
                        start=((c, r) == (0, 0)),
                        stop=((c, r) == (PLANES - 1, 0)),
                        is_transpose=True,
                    )

        def finish_rows(b):
            turn(range(HALF, PLANES), 0, [b])
            nc.scalar.activation(
                out=dh_rows[b][:], in_=turned[b][:].rearrange("p (m t) -> p t m", t=PACK), func=COPY, scale=lead[:, b : b + 1]
            )

        da_grouped = [
            keep.tile([P, n, PACK], BF16, name="da_grouped", tag="bf16_piece%d" % n0, align_bytes=64) for n0, n in PIECES
        ]
        da_codes = keep.tile([P, T], U32, name="da_codes", align_bytes=64)
        da_scales = keep.tile([P, T], U8, name="da_scales", align_bytes=64)
        results = [keep.tile([P, PACK, nb * P], F32, name="result%d" % b0, align_bytes=256) for b0, nb in CHUNKS]
        rounded = [
            keep.tile([P, nb * P, PACK], BF16, name="rounded", tag="bf16_piece%d" % (b0 * P), align_bytes=64)
            for b0, nb in CHUNKS
        ]

        def columns(k):
            n0, n = PIECES[k]
            return slice(n0, n0 + n)

        def result_of(k):
            n0, n = PIECES[k]
            at = n0 % (2 * P)
            return results[n0 // (2 * P)][:, :, at : at + n]

        backs = {}

        def make_da(k, a_sb):
            n0, n = PIECES[k]
            step = min(n, P)
            for at in range(n0, n0 + n, step):
                b = at // P
                if b not in backs:
                    backs[b] = bank(BACK_BANKS[b], [P, PACK, P])
                    for t in range(PACK):
                        nc.tensor.transpose(backs[b][:, t, :], dh_rows[b][:, t, :], ident[:])
                nc.vector.scalar_tensor_tensor(
                    out=da_grouped[k][:, at - n0 : at - n0 + step, :],
                    in0=a_sb[:, :, at : at + step].rearrange("p t n -> p n t"),
                    scalar=0.0,
                    in1=backs[b][:, :, at % P : at % P + step].rearrange("p t n -> p n t"),
                    op0=MAX,
                    op1=MULT,
                )

        def quantize_da(k):
            nc.vector.quantize_mx(
                out=da_codes[:, columns(k)].bitcast(FP8X4),
                scales=da_scales[:, columns(k)],
                in_=da_grouped[k][:].rearrange("p n t -> p (n t)"),
            )

        def project(k):
            width = PIECES[k][1]
            per_bank = min(PACK, BANK // width)
            for t0 in range(0, PACK, per_bank):
                acc = bank(OUT_BANKS[k][t0 // per_bank], [P, per_bank, width])
                for t in range(t0, t0 + per_bank):
                    nc.tensor.matmul_mx(
                        out=acc[:, t - t0, :],
                        lhsT=w1_codes[:, t * P : (t + 1) * P].bitcast(FP8X4),
                        lhsT_scale=w1_scales[:, t * P : (t + 1) * P],
                        rhs=da_codes[:, columns(k)].bitcast(FP8X4),
                        rhs_scale=da_scales[:, columns(k)],
                        start=True,
                        stop=True,
                    )
                nc.scalar.copy(out=result_of(k)[:, t0 : t0 + per_bank, :], in_=acc[:])

        def store(chunk, rows):
            b0, nb = CHUNKS[chunk]
            nc.sync.dma_start(
                out=out_0.rearrange("(p t) n -> p t n", t=PACK)[:, rows, b0 * P : (b0 + nb) * P],
                in_=results[chunk][:, rows, :],
            )

        def quantize_result(chunk):
            b0, nb = CHUNKS[chunk]
            cols = slice(b0 * P, (b0 + nb) * P)
            nc.vector.tensor_copy(
                out=rounded[chunk][:].rearrange("p (c i) t -> p c t i", i=4),
                in_=results[chunk][:].rearrange("p t (c i) -> p c t i", i=4),
            )
            nc.vector.quantize_mx(
                out=out_codes[:, cols].bitcast(FP8X4),
                scales=out_scales[:, cols],
                in_=rounded[chunk][:].rearrange("p n t -> p (n t)"),
            )

        def store_scales(queue, q, cols):
            queue.dma_start(
                out=out_2[0, 4 * q : 4 * q + 4, cols].bitcast(I32), in_=out_scales[32 * q : 32 * q + 4, cols].bitcast(I32)
            )

        def load_scales(q):
            nc.sync.dma_start(
                out=dy_scale_sb[32 * q : 32 * q + 4 * PASSES, :].bitcast(I32),
                in_=dy_scales[:, 4 * q : 4 * q + 4, :].bitcast(I32),
            )

        nc.vector.memset(dy_scale_sb[:].bitcast(I32), 0)
        first = {(0, 0): load_rows(w2t[0, 0:K_PASS, :], 0, PLANES)}
        nc.sync.dma_start(out=dy_word_sb[:], in_=dy_words.rearrange("s p n d -> p s (n d)").bitcast(I32))
        nc.sync.dma_start(offs_sb[:], offs)
        for q in range(4):
            load_scales(q)
        make_identity(nc, ident[:])
        for g in range(SLOTS // GATHER):
            gather_dy(g)

        expert_group(*GROUPS[0], 0, PLANES, 0, first)
        nc.sync.dma_start(pos_sb[0][:], pos1)
        nc.sync.dma_start(pos_sb[1][:], pos2)
        spread_gates()
        expert_group(*GROUPS[1], 0, PLANES, 4, {})
        expert_group(*GROUPS[2], 0, PLANES, 0, {})
        expert_group(E - 2, E - 1, 0, HALF, 4, {})
        expert_group(E - 1, E, 0, HALF, 6, {})
        expert_group(E - 2, E, HALF, HALF, 0, {})
        w1_raw = load_rows(w1t, 0, PLANES)
        a_sb = stage_tile([P, PACK, T])
        nc.sync.dma_start(out=a_sb[:].rearrange("p t n -> p (t n)"), in_=a.rearrange("(p t) n -> p (t n)", t=PACK))

        for c in range(HALF):
            for r in range(2):
                fetch_weighted(c, 1, r, 0, BLOCKS)
                turn([c], r, range(BLOCKS))
        fetch_plain(2, *CHUNKS[0])
        fetch_plain(3, *CHUNKS[0])
        fetch_weighted(HALF, HALF, 1, *CHUNKS[0])
        turn(range(HALF, PLANES), 1, (0, 1))
        fetch_plain(2, *CHUNKS[1])
        fetch_plain(3, *CHUNKS[1])
        finish_rows(0)
        finish_rows(1)
        fetch_weighted(HALF, HALF, 1, *CHUNKS[1])
        fetch_weighted(HALF, HALF, 1, *CHUNKS[2])
        fetch_onto(2, *CHUNKS[2])
        fetch_onto(3, *CHUNKS[2])
        make_da(0, a_sb)
        turn(range(HALF, PLANES), 1, (2, 3))
        w1_grouped = keep.tile([P, K * PACK], BF16, name="w1_grouped", tag="first30", align_bytes=64)
        for copy, words in ((nc.scalar.copy, slice(0, P // 2)), (nc.vector.tensor_copy, slice(P // 2, P))):
            copy(
                out=w1_grouped[:].rearrange("p (t m j) -> p m j t", t=PACK, j=PACK)[:, words],
                in_=w1_raw.rearrange("p j (m t) -> p m j t", t=PACK)[:, words],
            )
        for b in range(2, BLOCKS):
            finish_rows(b)
        quantize_da(0)
        nc.vector.quantize_mx(out=w1_codes[:].bitcast(FP8X4), scales=w1_scales[:], in_=w1_grouped[:])
        make_da(1, a_sb)
        project(0)
        store(0, slice(0, 2))
        store(0, slice(2, PACK))
        quantize_da(1)
        for k in (2, 3):
            make_da(k, a_sb)
            quantize_da(k)
        words_out = out_1[0].rearrange("p n d -> p (n d)").bitcast(I32)
        head = CHUNKS[0][1] * P
        quantize_result(0)
        nc.sync.dma_start(out=words_out[:, 0:head], in_=out_codes[:, 0:head])
        store_scales(nc.sync, 0, slice(0, head))
        project(1)
        store(1, slice(0, 2))
        store(1, slice(2, PACK))
        project(2)
        project(3)
        store(2, slice(0, PACK))
        quantize_result(1)
        quantize_result(2)
        nc.sync.dma_start(out=words_out[:, head:], in_=out_codes[:, head:])
        for q in range(4):
            store_scales(nc.sync, q, slice(head if q == 0 else 0, T))
